import numpy as np, ml_dtypes
CORES = [88,96,104,112,120,216,224,232,240,248]
N = 10
TOK, K, FT = 512, 3, 1
ROUTE = [[[1,3,4],[1,2,9],[1,8,9],[1,5,8],[1,5,9],[2,3,4],[1,7,8],[4,6,7],[0,2,3],[0,2,7],[4,6,8],[2,6,8],[0,7,8],[0,4,9],[1,5,7],[3,4,6],[0,1,6],[0,5,6],[3,6,7],[4,7,9],[3,4,9],[0,4,9],[3,4,7],[2,4,8],[1,5,7],[1,8,9],[1,3,8],[3,8,9],[1,2,7],[2,4,5],[4,5,7],[1,3,9],[3,7,9],[3,5,7],[0,3,7],[1,2,5],[3,7,8],[0,5,7],[0,5,8],[1,4,6],[0,4,8],[3,5,6],[0,1,4],[0,8,9],[0,1,3],[0,2,9],[1,4,8],[4,6,7],[3,4,6],[4,6,7],[4,7,9],[2,5,8],[2,7,8],[3,5,9],[1,2,8],[0,6,9],[1,7,8],[1,4,5],[0,5,8],[4,6,8],[0,2,9],[5,6,9],[2,5,8],[1,6,8],[1,7,9],[4,6,7],[4,6,8],[2,3,8],[0,1,3],[3,4,7],[2,8,9],[0,6,8],[2,6,7],[6,8,9],[0,2,8],[0,1,7],[3,7,8],[0,5,7],[0,4,6],[5,6,9],[0,1,9],[4,6,8],[0,7,8],[0,3,5],[0,4,8],[0,4,6],[2,3,5],[3,7,8],[1,2,9],[0,2,4],[6,7,8],[4,5,6],[2,8,9],[1,3,6],[0,1,9],[2,4,9],[3,4,7],[1,3,4],[2,6,9],[0,5,7],[3,4,9],[4,5,6],[1,2,8],[4,5,6],[3,6,9],[6,7,8],[3,6,9],[4,7,9],[4,6,7],[1,3,8],[0,2,8],[0,6,9],[0,6,7],[0,3,5],[0,3,6],[0,2,9],[0,3,4],[2,4,6],[0,5,6],[0,4,6],[0,5,6],[3,5,9],[0,3,6],[3,4,5],[4,7,8],[2,4,9],[1,5,7],[2,3,6],[2,4,6],[1,4,6],[3,6,7],[1,5,8],[1,2,8],[1,3,8],[3,7,8],[1,6,8],[0,5,8],[4,7,9],[0,6,9],[2,7,8],[1,6,7],[2,5,9],[2,4,8],[3,7,8],[3,6,8],[4,5,8],[0,2,7],[3,4,5],[0,1,9],[0,3,6],[5,6,7],[0,5,7],[0,5,8],[2,5,8],[0,1,5],[1,8,9],[1,6,7],[2,5,8],[2,4,6],[0,3,6],[0,2,4],[0,4,9],[3,5,9],[0,1,6],[1,3,4],[1,2,8],[1,6,9],[3,5,6],[0,2,7],[2,3,8],[1,4,5],[4,7,9],[0,3,5],[1,4,8],[4,7,8],[0,2,4],[2,5,6],[1,2,4],[5,6,8],[0,2,9],[1,2,9],[3,7,8],[1,5,6],[0,5,8],[1,6,8],[1,2,3],[0,5,7],[3,6,8],[6,7,8],[0,4,7],[0,6,7],[1,4,8],[1,2,8],[0,3,7],[2,3,5],[1,4,5],[0,4,8],[2,4,6],[0,3,6],[0,4,6],[0,3,5],[0,4,6],[3,8,9],[1,4,8],[0,3,7],[1,2,7],[0,1,5],[1,7,8],[1,7,9],[5,6,7],[2,8,9],[0,3,8],[0,1,8],[2,3,7],[0,2,7],[3,4,7],[0,8,9],[1,2,3],[3,4,5],[0,2,4],[0,3,9],[1,3,9],[2,4,7],[6,7,8],[1,3,6],[0,2,4],[0,3,4],[0,5,6],[3,4,6],[3,4,9],[3,6,7],[1,4,5],[0,6,8],[3,6,9],[6,7,9],[2,5,9],[1,4,5],[2,3,6],[1,4,5],[1,2,9],[1,4,6],[3,5,6],[0,7,8],[3,4,5],[0,4,8],[3,4,7],[2,5,8],[3,4,5],[4,6,9],[0,7,9],[1,5,6],[0,3,9],[1,2,6],[2,4,8],[2,4,8],[4,7,9],[0,6,8],[0,7,9],[2,6,8],[0,3,9],[0,1,3],[3,6,7],[4,6,9],[0,6,7],[1,4,5],[1,3,6],[3,4,9],[5,6,7],[1,3,4],[0,3,8],[1,7,8],[3,6,8],[2,5,9],[1,3,8],[0,7,8],[4,7,8],[2,6,7],[0,2,7],[2,5,7],[0,7,8],[3,4,6],[2,7,8],[3,4,7],[1,3,5],[0,3,6],[5,6,8],[0,5,9],[6,7,9],[0,2,4],[1,3,4],[0,2,9],[5,8,9],[7,8,9],[4,7,8],[3,4,8],[2,5,9],[3,7,8],[1,2,6],[2,6,9],[2,6,8],[3,4,6],[5,8,9],[0,2,8],[2,3,6],[6,8,9],[2,5,9],[0,2,5],[2,3,4],[3,6,9],[1,2,5],[0,1,2],[5,6,8],[0,2,6],[3,7,9],[2,6,9],[2,4,9],[0,2,4],[2,3,7],[0,1,4],[1,7,9],[2,5,6],[2,6,7],[2,5,7],[0,5,8],[1,4,6],[1,5,9],[3,4,9],[1,2,3],[0,1,9],[0,1,8],[0,3,5],[1,3,6],[5,7,8],[3,4,5],[3,7,8],[3,7,9],[1,2,5],[0,6,9],[1,3,9],[3,5,7],[0,1,9],[2,3,9],[0,1,8],[2,3,8],[6,7,8],[2,3,5],[1,2,9],[0,4,8],[1,5,6],[1,4,8],[0,2,3],[0,5,8],[0,2,8],[0,1,7],[0,1,6],[1,3,4],[6,7,9],[5,6,9],[3,5,7],[1,2,3],[3,4,5],[2,3,5],[6,7,9],[0,4,8],[2,5,8],[2,7,8],[0,1,3],[1,7,8],[1,5,8],[1,3,9],[3,4,7],[2,3,7],[2,4,7],[5,7,8],[4,8,9],[0,2,6],[2,4,5],[3,4,8],[1,4,9],[4,6,7],[4,7,8],[2,5,9],[0,7,8],[3,6,9],[4,5,7],[3,4,6],[2,5,7],[0,1,5],[0,1,5],[0,1,9],[0,1,7],[2,3,6],[2,5,8],[3,4,6],[2,3,8],[6,7,9],[3,4,5],[2,5,7],[4,5,8],[0,1,4],[0,1,7],[1,3,8],[0,2,3],[3,6,8],[0,3,8],[2,5,9],[0,2,3],[0,3,5],[0,2,4],[5,8,9],[5,6,9],[2,4,9],[0,4,8],[4,7,9],[0,1,7],[2,8,9],[3,5,7],[1,2,7],[3,4,6],[0,6,8],[0,1,2],[0,3,5],[2,3,5],[0,1,4],[5,6,9],[0,8,9],[0,3,6],[1,6,9],[1,2,7],[2,3,5],[0,1,6],[3,4,5],[0,8,9],[0,4,5],[1,4,9],[0,3,5],[4,6,9],[0,2,5],[0,5,7],[4,8,9],[0,3,9],[2,7,8],[0,2,8],[0,6,8],[0,3,5],[5,7,9],[3,4,8],[4,5,6],[1,3,6],[0,2,9],[0,3,9],[2,3,8],[0,5,8],[2,4,7],[7,8,9],[6,7,8],[4,6,7],[2,6,8],[2,3,8],[1,3,9],[4,5,8],[2,4,5],[0,4,6],[1,4,6],[2,4,9],[0,4,6],[1,2,9],[2,4,8],[3,4,9],[0,2,4],[0,5,6],[5,6,8],[0,8,9],[1,6,9],[5,8,9],[2,5,6],[1,3,5],[0,1,9],[1,5,9],[2,4,5],[5,7,9],[2,3,9],[1,6,9],[0,4,5],[1,6,9],[1,4,9],[0,1,9],[6,8,9],[3,6,9],[0,5,9],[0,3,7],[4,6,7],[0,5,8],[3,4,6],[1,6,7],[6,7,9],[0,6,9],[6,7,8],[1,5,7],[0,6,7],[0,5,9],[1,4,7],[0,1,2],[1,2,6],[3,5,6],[4,6,9],[0,3,5],[1,8,9],[0,4,9],[0,3,4],[1,6,9],[1,4,9]],[[2,7,8],[1,6,7],[2,3,9],[1,3,9],[1,6,9],[0,1,5],[0,1,5],[0,1,8],[3,5,9],[1,2,8],[1,5,9],[2,5,8],[4,6,8],[6,7,9],[0,5,8],[2,3,5],[1,5,8],[3,5,8],[3,4,6],[0,3,7],[2,5,9],[0,7,8],[2,5,8],[1,4,8],[0,5,9],[1,5,8],[6,8,9],[1,2,4],[0,1,3],[1,6,7],[0,1,4],[1,3,6],[0,4,7],[6,8,9],[1,4,6],[1,3,4],[5,7,8],[2,4,6],[0,2,4],[0,5,6],[5,7,9],[1,8,9],[0,7,9],[2,4,8],[0,6,7],[4,6,9],[0,6,7],[1,4,6],[1,6,7],[0,5,8],[1,4,8],[5,8,9],[0,2,9],[1,7,8],[0,8,9],[3,6,8],[2,4,7],[2,6,7],[0,3,9],[2,4,5],[0,3,8],[0,4,7],[6,8,9],[1,2,6],[0,4,7],[1,2,3],[2,4,7],[6,7,9],[3,8,9],[2,5,9],[2,3,5],[3,6,9],[0,5,9],[0,2,5],[1,3,7],[4,5,9],[3,4,7],[4,5,7],[3,4,7],[0,1,6],[2,3,8],[1,6,9],[0,2,4],[4,5,8],[2,3,7],[0,2,5],[2,7,8],[1,3,4],[6,7,9],[0,3,4],[0,2,9],[3,7,9],[3,4,9],[3,7,9],[0,1,9],[2,5,9],[0,3,8],[2,5,7],[2,4,5],[6,7,9],[3,6,9],[0,3,6],[1,8,9],[2,7,8],[0,2,7],[0,6,9],[4,5,8],[3,4,8],[3,6,9],[0,5,8],[0,2,3],[2,5,9],[1,2,6],[1,4,5],[0,5,7],[4,8,9],[3,5,9],[2,6,8],[0,7,8],[0,2,5],[0,4,8],[2,3,9],[4,7,9],[0,2,3],[4,6,9],[3,4,6],[1,5,8],[1,4,5],[1,3,8],[0,4,9],[2,5,7],[0,5,6],[3,4,8],[0,4,8],[2,5,8],[6,7,8],[5,8,9],[4,5,7],[1,2,5],[2,3,7],[0,3,9],[0,4,8],[0,2,7],[2,5,6],[3,5,6],[0,1,4],[0,5,9],[3,5,8],[1,3,5],[4,5,7],[5,6,8],[1,5,6],[2,6,7],[5,6,9],[7,8,9],[2,3,7],[3,6,7],[0,4,5],[2,4,7],[2,3,4],[0,4,5],[1,3,5],[0,4,5],[1,2,5],[1,4,8],[1,7,9],[1,2,3],[7,8,9],[3,6,8],[3,8,9],[0,2,5],[0,4,8],[3,6,7],[2,7,9],[2,4,9],[0,6,8],[3,5,9],[2,4,6],[4,5,9],[3,7,9],[0,3,8],[1,3,6],[0,1,9],[4,5,7],[2,4,5],[3,7,9],[4,5,7],[1,5,9],[0,4,8],[1,3,4],[1,8,9],[0,1,6],[1,4,8],[0,1,5],[2,8,9],[3,4,5],[5,6,9],[2,4,5],[1,5,7],[0,2,5],[2,6,9],[0,1,3],[3,6,9],[1,4,7],[2,6,8],[3,5,6],[2,7,8],[0,8,9],[1,8,9],[1,8,9],[2,5,7],[0,2,4],[2,4,6],[3,5,8],[2,4,9],[2,3,5],[3,5,9],[2,5,6],[1,3,8],[1,7,8],[3,4,8],[0,3,4],[4,6,7],[0,6,8],[0,1,2],[2,6,8],[3,4,8],[2,6,7],[4,5,7],[0,6,7],[0,5,6],[0,2,3],[1,3,6],[3,8,9],[5,7,9],[2,3,4],[1,3,7],[1,2,4],[0,2,3],[0,2,4],[1,6,9],[3,6,8],[0,3,9],[2,5,6],[4,8,9],[0,2,3],[1,2,4],[3,6,8],[3,4,9],[3,4,6],[2,3,7],[1,2,4],[3,5,7],[0,7,8],[1,2,4],[4,7,8],[1,4,6],[2,5,9],[0,2,5],[1,2,3],[3,8,9],[2,3,7],[2,8,9],[7,8,9],[4,5,6],[0,3,8],[0,2,7],[0,7,9],[4,5,9],[1,6,8],[0,5,9],[0,4,8],[2,6,8],[5,6,9],[0,5,7],[4,8,9],[1,3,4],[3,6,9],[3,8,9],[0,2,5],[1,5,9],[3,4,7],[3,4,7],[2,5,8],[0,1,4],[2,4,7],[0,1,7],[5,8,9],[2,5,7],[6,7,8],[1,2,9],[1,5,9],[0,1,6],[2,3,4],[3,6,7],[3,4,7],[0,6,8],[1,5,8],[0,3,4],[3,4,6],[3,4,9],[2,4,5],[3,6,8],[1,2,7],[5,7,8],[0,3,9],[0,1,6],[1,7,9],[3,5,9],[0,3,7],[1,2,9],[0,1,3],[0,3,4],[0,7,9],[2,4,6],[1,2,4],[6,7,8],[0,1,7],[0,1,4],[0,3,4],[0,3,7],[5,6,8],[4,5,6],[0,3,9],[2,6,8],[1,7,8],[1,3,7],[4,7,9],[0,4,6],[0,5,9],[3,8,9],[2,3,4],[1,8,9],[0,4,9],[2,7,9],[2,3,4],[4,8,9],[0,1,8],[0,1,2],[1,7,8],[1,3,7],[1,2,4],[2,3,4],[4,7,8],[3,4,7],[2,5,9],[5,6,9],[2,3,8],[1,6,7],[2,3,7],[0,4,5],[0,1,8],[4,8,9],[0,7,8],[1,8,9],[2,6,9],[0,5,8],[1,5,9],[2,4,6],[2,5,8],[2,3,9],[4,5,7],[0,2,7],[2,6,8],[3,4,9],[2,8,9],[1,3,6],[4,6,8],[1,6,7],[2,3,9],[0,7,9],[0,5,6],[3,5,7],[0,6,7],[1,2,7],[2,3,5],[1,2,9],[1,5,9],[1,3,5],[0,1,3],[0,4,9],[1,6,9],[0,4,6],[2,8,9],[0,4,6],[0,5,8],[3,6,8],[2,6,8],[2,4,9],[0,5,9],[4,5,8],[0,5,6],[3,6,8],[1,6,9],[0,2,9],[4,7,9],[3,8,9],[4,5,8],[3,8,9],[0,1,6],[1,2,7],[1,4,5],[2,5,8],[2,4,6],[0,1,4],[4,5,8],[1,3,4],[0,2,6],[4,6,8],[2,3,7],[1,2,3],[3,6,7],[0,3,7],[0,5,7],[2,3,9],[1,5,8],[1,2,5],[0,8,9],[0,3,7],[1,2,6],[4,5,9],[0,7,9],[0,5,7],[1,7,9],[2,6,7],[6,7,9],[0,2,8],[2,3,5],[0,8,9],[1,4,8],[1,8,9],[4,7,9],[0,7,8],[0,1,9],[2,7,9],[4,8,9],[0,4,6],[3,6,9],[5,8,9],[3,4,9],[1,2,4],[1,4,5],[3,5,7],[2,5,8],[2,5,6],[1,3,9],[5,6,7],[1,4,7],[3,5,9],[1,2,6],[4,7,8],[4,8,9],[0,3,6],[2,3,8],[4,7,8],[2,3,6],[1,3,6],[0,1,2],[2,5,9],[3,5,7],[1,5,9],[4,5,6],[3,4,7],[3,6,9],[2,3,4],[1,2,4],[0,1,6],[2,3,8],[0,2,8],[2,3,5],[0,1,8],[1,5,8],[3,5,6],[5,6,8],[3,4,8],[1,2,7],[1,6,7],[2,3,7],[1,7,9],[0,6,8],[3,4,8],[5,6,9],[0,5,6],[0,4,7],[3,7,9],[3,8,9],[3,4,7],[0,3,4],[2,4,8],[1,4,5],[1,3,8],[1,2,6],[2,3,9],[3,4,9],[1,4,9],[0,1,8],[1,7,9],[0,2,8],[5,7,8],[0,8,9],[1,3,4],[3,6,8],[1,5,6],[1,3,4],[2,5,6],[3,5,8],[3,6,8],[4,8,9],[0,2,9],[0,3,7],[4,8,9],[2,3,5]],[[4,7,8],[0,2,6],[2,7,8],[2,4,9],[1,5,9],[1,4,8],[0,4,6],[1,5,7],[3,4,5],[0,3,8],[0,6,7],[1,6,9],[0,4,7],[4,8,9],[5,7,9],[6,8,9],[2,5,8],[2,3,6],[2,5,6],[1,4,9],[2,4,9],[4,5,7],[7,8,9],[0,3,9],[3,7,8],[0,5,6],[0,5,8],[3,5,9],[2,7,8],[2,3,9],[1,7,8],[0,5,8],[2,4,6],[0,3,4],[2,7,9],[0,3,9],[2,7,9],[0,3,7],[4,7,9],[4,5,8],[3,5,7],[0,2,3],[0,3,7],[1,6,7],[2,5,7],[1,3,8],[1,2,8],[0,3,5],[1,4,6],[2,5,9],[0,4,5],[1,7,9],[7,8,9],[6,7,8],[1,2,7],[2,8,9],[3,4,6],[2,7,9],[0,4,6],[2,7,8],[2,6,8],[0,3,9],[0,1,5],[1,8,9],[3,5,8],[2,5,7],[4,8,9],[4,7,8],[1,4,5],[4,5,9],[1,2,5],[0,4,8],[5,6,7],[3,6,8],[3,6,9],[7,8,9],[1,5,7],[1,2,3],[2,5,6],[2,3,6],[2,3,9],[2,4,9],[4,5,9],[4,5,6],[0,4,7],[1,5,9],[5,7,8],[0,2,5],[0,3,8],[0,1,6],[4,7,8],[1,8,9],[2,3,8],[0,2,5],[1,4,6],[2,5,6],[6,7,8],[3,5,6],[1,3,5],[1,4,8],[0,3,4],[1,2,4],[0,7,8],[4,5,9],[0,7,8],[2,3,8],[0,1,5],[0,3,9],[0,1,6],[5,6,7],[1,5,9],[0,8,9],[6,8,9],[2,3,9],[0,3,6],[3,8,9],[0,7,9],[1,2,7],[2,6,9],[0,3,9],[0,1,3],[0,7,8],[4,8,9],[0,4,7],[0,1,2],[0,1,2],[0,2,5],[1,2,7],[2,5,7],[2,6,9],[5,6,7],[2,3,5],[1,5,8],[0,7,8],[1,6,7],[1,3,7],[3,4,7],[2,7,8],[4,5,6],[1,5,6],[1,5,8],[3,6,7],[0,4,5],[2,6,7],[3,4,6],[6,8,9],[2,5,6],[5,6,7],[5,6,7],[0,1,9],[0,6,8],[0,4,5],[2,3,5],[4,8,9],[2,8,9],[2,5,8],[0,5,6],[2,6,9],[4,7,8],[0,1,5],[0,5,7],[3,5,9],[4,6,9],[1,3,8],[1,3,4],[1,3,8],[0,5,9],[0,1,2],[0,8,9],[0,4,5],[0,3,5],[0,1,3],[3,6,9],[3,7,9],[1,2,4],[1,8,9],[5,7,8],[2,3,9],[3,4,8],[1,2,5],[1,6,8],[3,8,9],[1,3,6],[0,5,9],[2,5,9],[7,8,9],[2,8,9],[5,6,7],[1,5,9],[0,1,5],[6,7,9],[0,1,3],[0,6,9],[3,5,7],[3,7,8],[6,7,8],[0,3,9],[2,3,5],[3,6,7],[1,2,7],[2,3,7],[2,3,5],[1,4,8],[1,2,9],[5,6,7],[0,6,7],[1,8,9],[2,3,5],[0,2,3],[4,5,7],[0,7,9],[3,6,7],[0,4,6],[1,6,8],[2,4,8],[2,5,8],[3,7,9],[0,7,8],[4,6,9],[0,1,5],[0,3,5],[4,6,8],[0,2,8],[5,6,8],[1,3,9],[1,5,9],[1,2,3],[4,7,8],[0,4,6],[0,6,7],[1,6,7],[0,1,3],[5,6,7],[0,6,7],[3,7,9],[2,4,5],[3,6,9],[3,7,9],[0,8,9],[0,1,5],[4,5,7],[1,5,8],[2,4,9],[2,4,5],[1,3,9],[4,7,8],[1,2,9],[1,3,5],[2,8,9],[1,2,6],[2,3,9],[1,3,7],[4,6,9],[3,4,9],[1,7,8],[0,2,8],[3,7,9],[1,2,6],[1,2,3],[2,6,7],[1,5,9],[0,4,9],[3,5,6],[3,8,9],[1,4,7],[2,3,8],[1,8,9],[3,7,8],[1,5,7],[1,3,4],[1,4,9],[6,7,9],[0,1,2],[1,5,7],[1,3,8],[2,4,8],[2,5,7],[1,3,9],[2,6,7],[0,1,3],[4,5,8],[2,8,9],[3,5,9],[4,6,9],[5,6,8],[1,3,4],[1,2,5],[0,6,7],[3,4,8],[0,5,6],[2,4,7],[2,3,9],[1,2,4],[3,6,8],[0,2,6],[4,5,9],[0,3,7],[0,5,6],[2,7,9],[0,8,9],[0,2,9],[1,3,8],[3,5,7],[5,7,8],[0,1,2],[1,3,9],[1,3,8],[0,6,8],[0,3,8],[7,8,9],[1,2,9],[2,8,9],[0,4,7],[0,1,6],[2,4,8],[0,4,5],[1,3,9],[0,1,4],[1,4,8],[1,7,9],[2,3,9],[1,6,7],[1,5,7],[2,6,9],[1,2,7],[2,8,9],[0,3,5],[3,4,5],[1,4,8],[2,5,6],[0,1,4],[1,5,6],[5,6,9],[1,2,6],[0,1,8],[4,5,8],[1,6,7],[0,6,7],[0,3,8],[0,2,5],[0,4,8],[4,6,9],[1,3,6],[1,3,6],[6,7,8],[0,1,5],[2,5,6],[0,1,7],[1,3,5],[0,3,6],[2,4,5],[3,4,9],[2,3,9],[0,1,9],[3,6,7],[2,3,4],[0,1,5],[3,4,5],[5,6,7],[1,5,8],[0,4,5],[1,4,6],[0,2,8],[1,5,7],[2,6,9],[4,5,8],[4,7,9],[4,5,9],[2,5,6],[0,2,3],[3,7,8],[3,5,7],[5,6,8],[6,7,9],[0,1,3],[2,3,6],[0,3,9],[0,4,7],[2,3,6],[2,7,9],[1,5,7],[2,4,7],[2,7,9],[1,8,9],[2,3,7],[1,2,3],[0,5,7],[1,3,7],[1,8,9],[5,6,7],[1,6,8],[1,5,9],[4,7,8],[4,5,6],[0,5,6],[2,4,5],[3,7,8],[0,3,5],[4,7,8],[0,2,3],[2,4,7],[3,5,9],[2,7,9],[0,1,2],[1,4,6],[0,7,9],[2,3,6],[1,2,9],[1,3,5],[0,3,9],[0,2,7],[0,5,8],[0,2,7],[4,5,6],[0,5,8],[2,3,9],[0,7,9],[0,4,9],[0,5,8],[1,5,6],[6,7,9],[3,6,7],[0,5,8],[2,3,8],[0,3,8],[0,2,3],[1,2,3],[1,6,9],[0,3,5],[2,3,4],[5,7,8],[3,6,8],[0,2,3],[0,3,6],[0,2,7],[2,4,8],[1,5,9],[0,4,6],[0,1,9],[0,3,7],[2,3,9],[2,5,9],[0,4,7],[3,7,9],[4,5,7],[1,7,8],[3,6,7],[2,5,6],[1,4,7],[1,3,5],[0,3,7],[4,8,9],[1,6,8],[1,2,9],[1,3,9],[3,7,8],[0,2,3],[5,8,9],[0,5,7],[6,7,9],[1,2,6],[5,6,9],[4,6,8],[2,7,8],[0,1,7],[1,2,5],[1,8,9],[1,2,5],[0,5,8],[0,3,7],[2,5,7],[1,2,4],[1,6,9],[4,7,8],[2,3,6],[3,4,8],[1,2,6],[2,4,5],[0,1,4],[1,5,7],[2,6,9],[1,2,8],[2,3,6],[0,2,7],[0,1,2],[0,2,4],[2,3,6],[2,5,7],[0,1,3],[0,1,8],[1,4,9],[0,2,3],[0,2,5],[3,6,7],[0,3,5],[0,6,8],[0,2,8],[0,3,5],[0,6,7],[4,6,9],[0,7,8],[3,5,7],[0,3,6],[5,6,7],[1,2,9],[0,7,9],[0,8,9],[3,4,9],[0,2,5],[7,8,9],[1,2,3],[1,4,8]],[[1,6,8],[6,7,9],[2,4,7],[1,4,9],[0,3,8],[4,7,9],[6,8,9],[0,4,6],[0,1,4],[1,3,9],[0,2,7],[0,1,4],[3,5,9],[1,3,6],[2,7,9],[1,4,6],[0,7,9],[2,5,9],[5,7,8],[2,6,7],[0,1,7],[0,7,8],[0,1,9],[2,5,8],[0,8,9],[1,2,9],[2,8,9],[3,5,9],[0,5,9],[3,4,5],[0,5,9],[1,5,8],[2,3,7],[0,6,8],[0,2,5],[1,3,7],[2,4,6],[0,2,7],[0,5,7],[3,5,7],[5,6,9],[2,3,8],[0,3,6],[0,4,7],[1,2,8],[3,4,8],[4,7,9],[3,4,8],[3,4,5],[1,4,8],[5,8,9],[3,5,8],[2,3,9],[6,7,8],[0,1,7],[0,8,9],[0,1,6],[5,6,7],[3,7,8],[3,6,8],[1,3,6],[2,8,9],[3,5,8],[3,8,9],[1,8,9],[3,5,8],[4,5,9],[0,2,3],[1,4,7],[0,4,8],[1,2,7],[2,4,6],[6,8,9],[1,5,8],[2,6,8],[1,5,9],[3,4,6],[1,2,6],[2,8,9],[1,8,9],[0,2,7],[0,6,9],[5,7,9],[1,5,7],[2,4,6],[4,8,9],[1,4,5],[0,2,3],[4,8,9],[0,4,6],[0,3,6],[0,4,5],[2,3,5],[3,4,7],[3,7,8],[0,4,8],[6,8,9],[1,6,9],[5,6,8],[3,5,9],[2,5,9],[3,5,6],[2,5,6],[4,8,9],[2,6,7],[0,3,6],[4,5,7],[7,8,9],[1,4,9],[5,6,9],[4,7,8],[1,6,8],[5,6,7],[0,2,8],[0,7,9],[1,5,7],[2,7,9],[0,4,6],[4,6,7],[2,3,4],[0,6,9],[5,6,9],[3,7,9],[3,8,9],[1,2,8],[1,6,8],[0,2,4],[0,7,8],[0,3,6],[0,2,7],[3,4,9],[0,2,5],[1,4,8],[4,7,9],[1,3,6],[5,8,9],[4,7,8],[0,4,6],[0,5,8],[1,7,9],[0,1,2],[0,6,9],[1,7,9],[0,2,5],[1,6,8],[2,7,9],[1,6,9],[5,6,8],[0,7,9],[0,2,5],[0,3,4],[2,3,7],[1,6,9],[2,8,9],[0,1,4],[5,7,9],[0,7,9],[3,5,7],[3,4,8],[2,3,8],[0,4,5],[2,5,6],[3,6,7],[3,4,5],[0,3,9],[0,4,5],[4,6,8],[3,7,8],[0,2,3],[1,3,8],[2,7,8],[4,8,9],[1,3,6],[0,4,6],[0,4,9],[0,1,6],[2,4,7],[1,3,6],[1,3,9],[1,2,5],[6,8,9],[0,2,6],[3,5,8],[5,6,8],[0,3,5],[1,4,5],[2,5,8],[0,5,6],[0,2,9],[4,5,8],[0,7,8],[1,4,5],[0,2,7],[5,7,8],[0,7,8],[0,7,9],[0,1,2],[0,1,8],[6,7,9],[3,7,9],[1,3,9],[0,7,9],[3,5,9],[5,6,9],[1,5,6],[0,2,5],[2,6,8],[2,5,6],[5,6,8],[1,3,9],[4,7,9],[4,8,9],[5,6,8],[3,5,7],[3,5,9],[1,2,7],[1,8,9],[1,3,5],[0,6,9],[4,5,6],[2,6,7],[5,7,9],[3,5,8],[1,4,6],[0,4,5],[0,3,6],[2,4,9],[1,5,7],[4,8,9],[0,3,7],[4,6,7],[1,3,7],[4,6,9],[0,3,9],[3,4,9],[0,5,6],[0,7,8],[0,1,3],[0,6,9],[1,4,8],[1,3,6],[1,3,8],[6,7,8],[3,4,7],[1,2,3],[0,3,7],[2,7,8],[1,4,8],[1,4,9],[3,4,9],[1,4,7],[1,4,6],[4,6,7],[0,6,8],[0,7,9],[1,2,4],[3,4,5],[1,3,9],[4,5,8],[2,7,8],[1,7,9],[0,5,9],[0,7,8],[0,2,8],[1,4,6],[0,1,6],[0,4,9],[3,5,8],[0,1,7],[3,6,8],[6,8,9],[2,3,9],[4,6,7],[1,5,8],[3,4,5],[1,4,6],[3,6,7],[5,6,7],[4,6,8],[0,3,5],[4,7,8],[5,6,9],[7,8,9],[2,6,7],[0,2,8],[6,8,9],[0,7,9],[1,6,7],[0,6,9],[4,6,7],[3,4,5],[0,2,7],[2,6,9],[1,5,6],[0,1,7],[0,3,6],[3,4,8],[0,1,5],[5,7,8],[2,6,8],[0,4,5],[0,6,8],[0,3,7],[0,2,3],[0,4,7],[0,6,7],[0,2,6],[1,2,5],[1,3,7],[1,4,7],[0,3,7],[1,5,9],[0,3,9],[0,5,8],[2,7,8],[2,5,8],[5,7,9],[0,8,9],[1,2,7],[1,3,7],[3,5,6],[1,3,8],[0,2,4],[3,5,9],[1,3,9],[1,3,5],[1,6,9],[2,5,6],[4,6,9],[2,4,5],[2,4,7],[0,3,6],[3,5,8],[1,2,6],[0,4,9],[0,6,9],[0,1,3],[2,8,9],[0,7,9],[1,3,4],[1,5,6],[6,7,8],[2,5,7],[2,4,5],[0,4,5],[1,7,9],[2,4,9],[0,2,4],[3,8,9],[3,4,7],[0,6,7],[2,3,4],[3,5,8],[2,5,7],[3,7,8],[0,5,6],[0,1,8],[3,4,5],[1,6,7],[0,3,5],[0,2,9],[2,8,9],[0,3,6],[1,4,6],[1,4,7],[1,5,7],[3,8,9],[5,6,9],[0,4,9],[4,6,8],[2,5,9],[0,3,9],[1,2,7],[2,7,9],[2,7,8],[1,5,6],[1,5,9],[3,4,5],[6,7,8],[5,7,9],[1,3,6],[1,5,8],[0,1,7],[1,4,9],[6,8,9],[1,5,6],[5,6,8],[1,2,5],[0,4,9],[1,2,5],[4,6,7],[0,1,4],[4,6,9],[4,6,7],[6,7,9],[2,4,5],[1,6,7],[0,5,8],[1,5,9],[0,4,9],[1,2,5],[5,7,9],[1,4,7],[2,5,8],[0,5,9],[2,5,8],[2,7,8],[0,6,7],[0,1,3],[0,1,2],[3,4,8],[4,6,8],[0,1,6],[0,1,4],[2,3,4],[0,3,6],[3,6,8],[6,8,9],[1,4,5],[2,5,9],[2,5,9],[1,2,9],[1,2,7],[1,4,8],[0,3,6],[0,7,8],[0,6,8],[0,7,8],[1,4,6],[7,8,9],[0,4,8],[0,5,7],[4,6,8],[0,1,5],[0,5,6],[2,3,9],[3,5,6],[3,6,9],[6,7,8],[0,3,9],[1,6,8],[1,2,9],[5,8,9],[2,8,9],[3,5,9],[5,6,8],[2,5,9],[1,3,7],[5,8,9],[2,3,7],[0,3,4],[2,3,9],[2,5,6],[1,3,8],[2,6,7],[0,5,7],[0,3,5],[0,2,8],[0,5,7],[4,6,9],[3,5,6],[4,5,6],[0,1,4],[0,1,7],[1,5,7],[1,7,9],[2,5,6],[2,3,4],[0,7,8],[3,4,9],[0,1,6],[0,1,9],[1,5,6],[1,5,9],[2,3,7],[4,6,7],[1,2,4],[2,8,9],[2,7,9],[4,5,6],[2,3,6],[4,5,7],[3,5,6],[3,7,9],[4,7,8],[0,1,8],[0,6,7],[1,2,8],[3,4,8],[6,7,9],[0,8,9],[3,5,8],[4,7,9],[5,7,8],[1,2,4],[0,7,8],[2,4,9],[1,2,4],[3,4,8],[1,3,9],[0,3,4],[0,1,7],[1,5,8],[5,6,7],[2,5,7],[0,5,6],[2,5,8],[2,3,6],[0,6,7],[2,3,7],[3,6,8],[5,6,8]],[[1,6,8],[0,1,2],[6,7,8],[2,3,5],[0,6,7],[2,3,7],[1,5,7],[3,4,7],[2,3,8],[0,3,7],[3,5,6],[0,4,6],[1,5,8],[2,7,8],[1,5,9],[0,2,7],[2,3,8],[1,3,8],[2,4,5],[3,4,8],[0,7,9],[0,5,6],[3,6,8],[2,5,9],[3,4,5],[1,3,5],[0,2,3],[0,4,8],[4,5,9],[0,7,8],[5,7,8],[2,5,7],[6,7,9],[4,8,9],[1,2,5],[2,4,9],[1,2,3],[0,1,4],[3,6,7],[2,5,8],[4,5,7],[2,4,8],[0,4,8],[1,7,8],[0,1,3],[3,5,6],[0,3,8],[0,4,5],[4,7,8],[0,6,8],[1,3,9],[0,2,7],[0,7,8],[0,3,9],[1,7,8],[0,1,9],[4,5,8],[1,2,3],[1,3,9],[1,3,7],[0,4,7],[5,6,8],[1,4,6],[1,7,9],[4,5,8],[0,7,9],[4,8,9],[0,2,5],[0,2,9],[1,2,3],[0,1,6],[0,6,8],[7,8,9],[0,4,8],[1,6,7],[1,2,5],[0,5,8],[0,3,9],[2,7,9],[0,7,8],[0,8,9],[4,7,9],[2,6,7],[5,6,7],[4,6,7],[4,5,7],[0,5,7],[1,3,5],[1,2,7],[0,3,4],[0,7,8],[1,2,4],[1,4,8],[3,6,9],[1,4,7],[0,3,6],[0,5,7],[3,5,9],[3,5,8],[1,2,4],[2,3,5],[0,3,9],[3,5,8],[0,5,9],[2,6,9],[0,1,3],[1,3,6],[4,5,9],[0,1,5],[0,1,9],[1,2,7],[3,5,8],[2,5,9],[1,2,3],[1,2,6],[3,5,7],[4,7,8],[1,2,4],[0,4,6],[2,3,8],[0,3,6],[1,5,9],[1,3,4],[1,4,8],[5,6,8],[3,6,7],[3,6,9],[2,4,5],[0,1,7],[0,2,5],[1,2,5],[1,3,4],[2,3,9],[1,6,7],[2,4,5],[0,5,9],[1,3,7],[3,6,7],[0,4,8],[1,3,7],[1,4,9],[4,6,7],[0,3,6],[2,5,7],[2,4,5],[1,2,4],[4,7,9],[3,5,8],[1,3,4],[0,6,8],[1,2,5],[2,4,7],[0,1,4],[0,2,5],[3,4,8],[2,4,5],[1,5,9],[0,2,9],[0,3,7],[5,6,7],[1,6,7],[0,1,4],[0,4,5],[5,7,9],[2,3,6],[1,8,9],[1,6,9],[2,6,7],[0,5,6],[3,4,7],[1,3,8],[0,2,8],[2,7,8],[1,7,8],[1,3,5],[0,2,7],[1,4,8],[0,4,8],[0,7,9],[0,4,7],[5,8,9],[0,1,6],[1,7,8],[3,8,9],[1,4,9],[1,2,7],[0,4,6],[1,2,3],[1,7,9],[1,5,6],[4,6,7],[0,4,8],[1,7,8],[1,5,6],[3,6,7],[2,3,8],[2,4,6],[3,4,9],[0,5,7],[5,6,8],[4,7,9],[3,6,8],[0,3,5],[1,2,8],[1,4,7],[1,8,9],[2,5,7],[0,6,9],[0,6,8],[3,7,9],[1,5,7],[2,7,9],[0,1,7],[1,3,8],[1,3,9],[4,8,9],[0,4,7],[1,2,4],[1,4,8],[7,8,9],[1,4,6],[2,6,7],[1,6,8],[0,3,7],[0,3,8],[4,7,8],[0,7,9],[1,6,8],[6,7,9],[0,4,9],[4,8,9],[1,2,6],[0,5,7],[0,1,7],[0,2,3],[1,5,7],[0,3,8],[0,4,9],[0,4,6],[2,6,9],[0,2,3],[1,2,3],[1,7,8],[1,5,8],[4,5,6],[5,6,7],[5,8,9],[5,6,8],[1,5,6],[1,2,3],[3,5,7],[0,3,5],[3,4,7],[0,4,6],[3,7,9],[0,3,8],[1,2,3],[6,7,8],[2,4,9],[2,4,8],[0,2,9],[1,4,6],[2,6,7],[1,7,9],[3,4,5],[0,2,6],[1,2,8],[1,2,9],[0,3,5],[2,5,7],[5,7,9],[2,5,9],[1,3,4],[2,3,9],[0,1,4],[3,6,9],[1,2,9],[2,6,8],[0,5,7],[0,3,6],[0,7,8],[1,7,9],[2,4,8],[0,4,6],[3,4,9],[1,2,4],[3,7,9],[1,4,5],[4,5,7],[1,4,7],[1,4,7],[6,8,9],[3,4,8],[2,6,7],[3,4,6],[6,7,8],[1,3,5],[0,2,4],[1,4,8],[0,1,5],[3,6,9],[0,4,6],[3,8,9],[0,1,6],[0,3,9],[2,7,9],[0,1,7],[6,7,9],[0,3,5],[0,4,9],[1,5,9],[4,6,9],[3,6,7],[0,2,7],[1,2,8],[3,4,9],[7,8,9],[1,3,6],[0,1,8],[0,1,4],[2,6,9],[2,5,9],[1,3,6],[1,3,7],[2,3,6],[6,8,9],[0,3,8],[0,1,5],[3,5,7],[1,2,5],[1,3,6],[2,5,6],[3,6,9],[3,4,6],[0,7,8],[2,5,9],[1,5,8],[1,4,8],[0,1,8],[2,4,5],[4,7,8],[2,3,4],[0,3,8],[1,3,9],[1,3,8],[0,1,3],[1,7,9],[5,7,8],[7,8,9],[2,6,9],[2,7,8],[2,6,7],[3,4,8],[0,4,8],[1,4,9],[0,2,3],[3,4,8],[1,2,3],[0,2,5],[0,5,8],[1,4,7],[0,4,9],[3,5,7],[1,3,8],[1,4,6],[0,6,8],[1,7,8],[0,3,8],[1,2,7],[5,7,8],[2,8,9],[1,2,9],[0,4,9],[1,4,9],[1,4,8],[1,3,5],[0,1,6],[5,6,7],[3,6,9],[0,4,7],[0,1,7],[1,2,8],[3,8,9],[0,1,8],[6,8,9],[0,2,7],[5,6,9],[3,4,5],[0,6,9],[3,4,9],[3,8,9],[0,5,6],[0,4,8],[1,3,6],[1,2,3],[2,3,8],[2,8,9],[1,5,9],[2,4,5],[1,5,9],[0,4,5],[0,4,7],[0,2,7],[2,4,5],[0,1,5],[0,8,9],[0,1,5],[2,3,4],[6,8,9],[0,3,9],[0,3,9],[4,6,8],[2,3,7],[1,2,8],[4,5,8],[1,5,9],[0,5,7],[0,8,9],[2,6,7],[4,5,7],[1,3,4],[4,7,9],[1,6,9],[2,6,9],[3,4,5],[3,5,8],[1,4,8],[2,8,9],[3,7,9],[1,2,6],[2,3,7],[2,3,6],[1,4,6],[2,5,6],[0,4,9],[3,7,8],[1,2,3],[3,8,9],[0,1,2],[4,5,9],[1,8,9],[0,6,9],[3,4,7],[2,7,9],[5,6,9],[5,7,9],[3,6,8],[0,6,8],[0,3,7],[5,6,7],[2,5,7],[3,8,9],[0,5,8],[1,2,4],[2,5,7],[1,6,8],[3,8,9],[0,2,3],[1,7,8],[2,3,4],[5,6,9],[1,3,4],[0,8,9],[0,1,5],[1,2,6],[6,7,9],[1,5,7],[1,2,7],[1,2,8],[1,2,7],[3,4,8],[1,2,9],[2,4,7],[3,4,7],[0,1,6],[0,5,9],[1,2,5],[1,3,9],[2,6,7],[1,2,6],[3,4,9],[2,3,9],[0,3,7],[6,8,9],[1,2,4],[1,4,9],[0,2,6],[0,5,8],[0,3,9],[3,5,7],[0,5,7],[0,6,8],[3,4,9],[1,3,4],[2,4,8],[1,6,8],[0,7,8],[0,1,6],[0,2,6],[5,6,8],[2,8,9],[3,5,7],[2,5,9],[0,8,9],[4,5,7],[0,4,8],[1,5,8],[0,6,7],[3,4,5],[0,2,4],[1,2,7],[3,4,7]],[[0,6,9],[1,5,8],[1,2,3],[2,5,9],[1,5,8],[0,3,9],[4,8,9],[2,6,7],[4,5,6],[3,6,7],[0,5,7],[1,5,6],[0,6,8],[0,2,3],[2,5,7],[1,3,8],[2,3,6],[0,2,9],[0,7,9],[1,2,8],[2,3,6],[0,3,5],[3,4,6],[1,2,9],[1,2,3],[2,7,9],[2,4,9],[0,3,6],[0,3,4],[1,2,8],[5,6,9],[2,5,9],[3,5,6],[0,7,8],[2,3,7],[6,7,8],[2,4,6],[1,6,7],[3,4,9],[4,5,8],[2,5,8],[3,4,7],[1,3,4],[0,1,3],[0,3,9],[1,2,9],[1,2,7],[0,2,3],[1,2,6],[0,1,5],[0,6,8],[1,2,4],[1,3,6],[2,3,7],[2,4,5],[6,7,8],[6,8,9],[1,3,8],[0,6,7],[0,7,9],[0,3,6],[2,3,9],[1,6,8],[2,3,7],[5,6,9],[1,2,8],[1,3,5],[3,4,6],[0,3,5],[0,7,8],[0,3,5],[2,4,6],[1,4,5],[1,4,5],[1,4,6],[0,3,8],[0,5,6],[6,7,9],[1,2,6],[0,3,5],[1,3,8],[0,1,7],[1,7,9],[4,6,8],[0,2,6],[2,3,6],[1,7,9],[1,5,7],[2,5,9],[0,1,5],[1,7,9],[5,6,7],[2,6,7],[3,7,9],[2,4,9],[4,6,7],[3,4,8],[3,7,8],[6,8,9],[5,8,9],[4,8,9],[7,8,9],[7,8,9],[2,3,4],[1,5,7],[0,3,7],[1,2,3],[0,4,9],[0,1,4],[1,3,6],[0,6,8],[0,1,5],[2,3,9],[3,5,7],[3,7,9],[1,4,5],[3,4,8],[1,2,4],[1,5,8],[3,4,9],[1,4,9],[6,8,9],[1,7,9],[0,5,7],[5,7,9],[3,7,9],[0,3,7],[0,2,5],[1,2,3],[3,6,9],[2,4,8],[5,6,9],[2,4,5],[1,7,8],[4,6,8],[1,3,4],[0,5,6],[3,6,7],[5,6,8],[4,7,9],[0,5,8],[1,7,8],[0,4,7],[3,4,5],[2,7,9],[2,6,8],[5,8,9],[1,3,5],[2,3,7],[4,5,6],[0,1,5],[1,2,3],[0,3,8],[3,4,8],[0,3,5],[0,7,9],[0,3,4],[0,1,9],[1,7,9],[5,8,9],[1,3,9],[3,4,8],[6,7,9],[1,3,5],[0,4,7],[3,4,9],[2,3,8],[2,3,6],[4,7,9],[2,5,8],[0,1,7],[0,2,3],[1,4,7],[2,4,9],[2,3,5],[0,1,9],[1,3,5],[0,2,9],[2,7,9],[1,2,4],[3,5,8],[0,1,5],[0,2,6],[4,5,6],[0,3,7],[2,5,8],[3,6,9],[2,6,9],[2,5,7],[1,2,7],[2,7,9],[1,8,9],[1,4,9],[0,5,6],[0,1,9],[0,4,9],[0,1,9],[0,6,9],[2,3,9],[0,3,5],[1,4,7],[0,6,9],[6,7,9],[4,7,9],[0,3,5],[4,5,7],[3,8,9],[1,2,5],[3,5,7],[0,2,4],[1,3,8],[0,2,5],[5,8,9],[0,6,8],[4,6,7],[3,7,9],[5,6,8],[0,2,8],[3,7,9],[3,8,9],[1,2,9],[6,8,9],[1,4,6],[2,8,9],[2,5,7],[2,4,7],[0,2,8],[3,6,7],[0,4,8],[0,1,2],[3,4,5],[0,3,5],[4,5,8],[2,7,9],[1,3,7],[6,8,9],[1,5,9],[3,4,9],[2,3,9],[5,6,8],[0,8,9],[0,1,6],[4,6,8],[0,4,5],[3,7,8],[3,4,7],[3,7,8],[0,7,9],[2,6,9],[0,5,8],[3,4,7],[0,2,4],[2,6,8],[3,8,9],[1,3,5],[5,6,7],[0,4,6],[0,1,3],[2,4,5],[0,6,8],[3,7,8],[5,7,9],[0,5,6],[2,4,7],[1,2,3],[0,1,7],[1,5,8],[3,6,8],[1,5,9],[2,4,8],[6,8,9],[1,7,8],[0,3,9],[1,6,8],[2,5,6],[1,2,6],[2,8,9],[0,3,4],[0,1,6],[1,4,8],[0,4,9],[1,8,9],[5,6,8],[1,5,6],[0,5,9],[5,6,9],[0,5,7],[2,3,9],[1,5,7],[3,4,8],[2,3,9],[2,3,7],[1,5,9],[2,4,8],[0,1,8],[0,1,2],[3,7,8],[0,8,9],[0,6,8],[0,5,6],[1,2,9],[2,4,7],[2,3,5],[2,6,9],[0,5,8],[0,5,7],[1,2,4],[4,6,7],[4,5,6],[2,6,7],[1,3,6],[0,1,3],[2,3,4],[3,5,8],[2,3,7],[2,3,5],[0,4,5],[1,2,3],[2,5,7],[3,4,7],[2,3,4],[0,1,6],[0,8,9],[0,5,6],[2,3,9],[4,5,6],[0,7,9],[3,7,9],[0,5,9],[1,3,7],[1,3,6],[4,5,7],[6,8,9],[0,6,7],[1,6,9],[0,3,5],[4,5,7],[3,4,8],[0,1,5],[0,3,8],[1,6,7],[0,2,8],[4,5,9],[2,4,7],[0,6,7],[0,3,5],[2,3,4],[2,6,8],[0,1,8],[2,3,9],[6,8,9],[0,7,8],[2,3,9],[3,4,7],[0,1,8],[0,1,5],[1,7,9],[0,4,9],[2,4,7],[2,7,8],[6,7,8],[4,5,9],[3,6,7],[4,8,9],[2,4,9],[1,4,8],[0,5,8],[0,6,7],[0,3,7],[1,3,7],[0,6,8],[1,3,4],[1,4,7],[3,6,8],[1,3,8],[2,3,8],[0,4,8],[3,6,9],[2,6,7],[0,4,8],[0,1,5],[0,2,4],[4,7,9],[1,2,3],[3,6,7],[4,6,8],[0,4,5],[0,1,9],[3,5,8],[0,1,9],[5,6,7],[0,2,4],[2,7,9],[3,5,8],[3,8,9],[1,6,8],[1,5,9],[3,8,9],[0,5,6],[0,2,5],[4,5,9],[5,6,8],[1,6,9],[0,4,8],[0,5,8],[1,5,9],[5,6,9],[1,2,7],[4,5,6],[5,7,8],[0,6,8],[2,6,9],[0,1,5],[3,6,7],[4,5,6],[3,6,7],[0,3,9],[2,5,8],[1,3,8],[2,5,8],[1,6,8],[0,2,6],[2,5,7],[1,6,8],[0,4,5],[1,4,7],[1,4,9],[2,5,9],[2,4,8],[1,5,9],[0,5,8],[4,5,8],[2,3,8],[0,5,7],[0,5,7],[1,5,8],[3,6,8],[5,6,8],[0,1,3],[3,5,6],[1,2,4],[0,6,7],[0,1,7],[0,4,5],[1,5,9],[1,2,7],[1,5,8],[1,8,9],[1,7,9],[1,4,9],[5,6,7],[6,7,8],[0,4,8],[2,7,8],[6,7,9],[1,4,6],[0,5,8],[2,3,5],[2,3,9],[0,7,9],[3,5,6],[3,6,8],[2,3,8],[0,4,6],[0,3,8],[2,3,7],[0,3,8],[4,7,8],[3,6,9],[4,5,9],[2,5,6],[0,3,9],[2,4,9],[2,5,7],[2,3,9],[1,7,9],[3,4,5],[1,5,9],[3,6,9],[4,5,7],[5,7,8],[0,6,7],[1,6,8],[0,5,9],[0,8,9],[2,3,9],[0,7,8],[1,5,8],[2,3,8],[0,6,9],[3,6,9],[2,3,4],[4,5,8],[4,7,8],[0,2,4],[4,7,8],[0,3,9],[4,6,9],[2,4,5],[0,1,8],[0,1,7],[2,7,8],[0,6,8],[0,6,9],[1,3,5],[2,4,9],[3,8,9],[0,3,4],[0,2,8],[2,6,8],[3,5,7],[2,3,4]],[[0,2,3],[1,8,9],[0,1,6],[1,2,9],[0,5,9],[0,1,7],[0,5,7],[1,4,7],[1,4,8],[0,5,9],[0,5,7],[1,2,4],[0,1,4],[0,1,7],[2,3,4],[0,2,3],[4,6,9],[2,8,9],[3,6,9],[4,6,7],[0,2,9],[4,8,9],[1,2,9],[0,3,7],[3,6,8],[4,5,7],[1,5,8],[3,8,9],[0,3,5],[2,4,6],[0,4,8],[3,4,7],[3,7,8],[4,8,9],[1,6,9],[1,3,8],[6,8,9],[6,7,8],[2,5,7],[1,7,9],[1,2,8],[2,8,9],[5,6,9],[3,6,9],[0,3,9],[2,4,6],[1,6,9],[0,1,8],[4,7,9],[1,3,5],[3,8,9],[3,6,9],[2,3,4],[2,3,5],[4,7,9],[1,5,9],[5,6,9],[4,6,9],[1,6,8],[0,6,7],[3,5,8],[2,4,9],[4,7,8],[2,3,4],[6,7,9],[1,5,9],[0,1,3],[1,3,5],[3,4,8],[0,8,9],[2,6,8],[1,3,5],[1,4,6],[0,3,4],[2,4,9],[0,3,7],[4,5,9],[4,6,7],[5,8,9],[1,2,7],[5,7,8],[3,4,6],[2,4,7],[1,4,9],[0,2,5],[2,4,5],[0,8,9],[2,3,4],[0,3,9],[4,5,7],[0,1,7],[0,5,6],[2,5,8],[2,6,9],[1,3,9],[0,2,7],[0,2,3],[1,5,7],[0,6,8],[2,3,5],[0,2,3],[1,5,7],[1,4,7],[0,2,8],[0,4,5],[1,2,7],[6,7,8],[0,4,5],[6,7,9],[2,3,8],[2,3,5],[6,7,9],[0,3,4],[2,5,6],[5,6,9],[2,4,7],[3,4,9],[2,3,6],[1,2,7],[1,7,8],[2,4,6],[2,4,7],[1,4,7],[4,5,7],[2,6,9],[0,4,7],[1,3,8],[1,4,9],[2,6,7],[1,5,7],[2,6,9],[1,6,7],[1,4,8],[2,4,5],[2,4,9],[1,4,6],[1,8,9],[0,4,8],[7,8,9],[3,7,8],[2,5,9],[1,6,8],[3,5,7],[0,3,6],[1,5,8],[1,6,8],[3,4,7],[0,2,3],[0,2,6],[0,3,6],[1,5,6],[5,6,7],[0,1,5],[0,5,7],[2,6,7],[0,2,5],[5,7,9],[0,1,6],[2,4,7],[5,8,9],[0,2,7],[4,5,6],[1,2,4],[3,6,8],[1,8,9],[0,5,6],[3,4,7],[0,1,7],[2,3,7],[3,4,9],[0,3,6],[0,2,8],[3,4,6],[4,5,8],[2,3,8],[0,1,8],[4,5,6],[0,1,5],[0,2,3],[2,3,5],[4,6,8],[1,2,7],[6,8,9],[4,7,8],[0,5,8],[2,4,5],[1,3,5],[0,1,3],[4,5,7],[5,6,7],[5,8,9],[3,5,6],[0,4,6],[6,7,8],[2,5,7],[3,5,6],[0,7,8],[1,6,9],[2,6,7],[5,8,9],[4,6,8],[4,6,7],[4,6,7],[0,2,5],[4,7,8],[0,3,4],[4,5,8],[1,5,9],[3,5,6],[3,7,9],[0,4,8],[0,1,8],[3,4,5],[4,5,9],[2,3,7],[0,1,2],[0,1,9],[3,4,6],[3,5,9],[2,7,8],[1,8,9],[4,6,8],[0,1,4],[0,6,9],[0,4,8],[1,2,6],[2,4,6],[0,1,4],[0,4,5],[3,5,9],[1,2,6],[4,7,8],[0,2,4],[1,3,5],[1,5,6],[0,4,8],[0,1,5],[1,6,9],[0,5,7],[2,3,7],[2,3,8],[3,5,7],[5,8,9],[0,1,9],[1,5,9],[2,5,6],[6,8,9],[1,6,8],[3,6,9],[4,5,6],[0,6,7],[0,3,6],[0,1,9],[1,4,7],[5,6,8],[0,2,8],[0,3,4],[1,2,6],[1,2,6],[0,5,7],[2,3,4],[0,2,5],[1,8,9],[1,6,7],[1,6,8],[1,2,8],[3,4,5],[0,1,9],[1,3,4],[6,7,8],[0,2,6],[3,6,8],[0,1,5],[0,1,8],[0,1,3],[4,8,9],[0,2,9],[3,6,9],[4,5,8],[2,3,9],[1,2,5],[0,4,7],[1,8,9],[0,5,8],[2,6,7],[0,3,9],[4,5,9],[1,2,3],[1,2,8],[0,3,7],[3,4,8],[0,4,7],[6,8,9],[6,7,9],[3,5,8],[0,4,8],[3,7,8],[5,7,9],[0,2,6],[0,4,8],[1,4,9],[0,5,8],[4,5,8],[2,8,9],[5,6,8],[1,2,6],[1,4,8],[0,4,6],[6,7,9],[2,7,9],[0,1,3],[1,4,9],[3,5,6],[4,5,8],[0,3,8],[2,6,7],[0,6,7],[0,6,7],[0,1,6],[0,4,5],[0,1,5],[2,7,9],[1,4,7],[2,4,7],[1,4,9],[2,5,7],[2,4,7],[1,2,6],[0,4,7],[4,6,7],[1,4,9],[2,7,9],[0,7,8],[3,5,8],[2,4,7],[3,6,9],[1,2,8],[0,2,3],[1,3,6],[2,3,7],[1,3,4],[2,5,9],[0,3,5],[0,4,7],[3,4,7],[0,3,5],[2,3,8],[4,6,9],[0,4,7],[1,5,8],[3,5,6],[1,7,8],[2,4,6],[3,6,8],[0,1,8],[0,1,2],[1,6,9],[0,4,6],[1,5,7],[3,4,6],[4,6,9],[5,6,7],[1,2,5],[0,8,9],[0,5,9],[1,5,8],[6,7,8],[0,2,7],[1,3,5],[2,4,5],[1,4,7],[0,1,8],[5,7,9],[1,5,9],[1,6,7],[2,6,9],[1,3,4],[0,1,7],[0,3,6],[0,4,7],[1,5,8],[3,5,7],[4,5,9],[0,4,5],[3,7,9],[4,5,7],[0,1,9],[0,3,7],[6,8,9],[3,5,7],[0,1,2],[4,5,9],[1,7,8],[2,5,8],[1,6,9],[0,1,2],[6,7,9],[0,2,6],[1,3,7],[3,5,8],[1,3,4],[1,2,4],[3,6,8],[4,5,7],[2,4,7],[4,6,8],[0,4,6],[5,6,7],[5,6,9],[2,5,9],[0,5,7],[0,2,6],[1,2,4],[4,7,8],[4,5,9],[2,4,5],[0,2,9],[2,4,8],[1,2,6],[3,4,9],[4,6,7],[0,1,2],[1,4,5],[2,5,9],[2,3,7],[1,5,9],[4,6,7],[7,8,9],[0,5,7],[2,4,9],[2,3,7],[1,3,6],[0,3,8],[0,5,8],[1,2,5],[0,8,9],[5,7,8],[1,3,5],[3,5,7],[5,6,8],[1,6,7],[0,6,9],[4,5,7],[0,2,6],[4,7,9],[7,8,9],[0,2,8],[0,8,9],[3,4,8],[2,3,7],[5,7,8],[0,2,7],[0,4,8],[0,5,9],[7,8,9],[5,7,8],[1,5,9],[0,1,4],[3,4,8],[1,7,9],[0,5,7],[1,2,5],[5,6,9],[0,4,8],[1,2,9],[1,3,6],[0,4,7],[1,4,6],[5,7,8],[1,4,9],[1,4,6],[2,3,4],[0,3,7],[1,6,8],[3,5,6],[3,5,9],[1,2,9],[2,3,9],[2,4,9],[3,6,9],[0,4,6],[1,2,9],[2,4,9],[4,5,6],[0,6,9],[3,6,9],[0,1,8],[0,4,5],[0,2,8],[2,5,7],[3,4,6],[4,5,9],[6,7,8],[1,4,6],[0,4,5],[0,2,8],[0,2,6],[3,4,8],[2,5,7],[4,6,8],[4,6,8],[1,4,8],[1,3,8],[2,5,6],[2,8,9],[6,8,9],[5,8,9],[1,2,8],[0,2,5],[1,2,9],[2,6,8],[1,6,8]],[[0,5,6],[2,5,9],[2,3,9],[0,2,6],[1,3,5],[0,4,6],[1,3,4],[2,5,7],[0,2,4],[2,4,8],[2,5,7],[3,5,8],[0,4,9],[4,5,7],[2,5,7],[0,2,3],[4,6,7],[4,6,7],[2,3,9],[2,7,9],[3,6,7],[1,2,5],[3,6,8],[2,3,9],[3,5,8],[2,3,8],[0,3,5],[0,3,4],[2,5,8],[1,5,9],[2,4,7],[1,3,8],[1,4,6],[3,4,7],[2,3,5],[2,6,8],[4,5,8],[0,5,8],[3,6,8],[7,8,9],[2,5,8],[4,5,8],[3,4,6],[1,5,9],[4,6,7],[2,7,8],[0,1,4],[0,5,6],[1,2,3],[0,1,5],[1,4,8],[2,5,6],[0,3,5],[4,8,9],[2,3,5],[0,2,8],[0,1,9],[0,4,6],[2,4,7],[1,7,8],[0,6,8],[1,4,8],[2,4,9],[0,2,4],[2,3,9],[4,6,9],[3,8,9],[7,8,9],[4,6,7],[0,2,5],[2,6,8],[0,1,3],[7,8,9],[3,4,8],[3,4,6],[5,6,7],[3,5,9],[1,7,9],[1,2,7],[0,4,9],[0,1,9],[2,4,7],[1,4,8],[0,4,8],[2,6,8],[2,5,8],[4,5,6],[2,4,9],[3,4,9],[1,2,9],[1,2,8],[0,1,9],[0,1,5],[3,7,8],[3,5,7],[0,4,5],[1,2,3],[2,4,5],[0,2,6],[0,4,6],[0,5,8],[0,3,6],[3,4,5],[4,6,7],[4,5,9],[1,3,9],[1,4,7],[3,5,8],[2,3,4],[1,2,7],[5,6,9],[1,4,7],[2,3,9],[0,3,9],[0,6,7],[1,3,9],[1,4,8],[0,2,4],[0,1,9],[1,4,9],[3,7,9],[1,3,9],[4,5,9],[6,7,9],[2,3,7],[2,5,8],[3,4,8],[1,3,9],[3,5,8],[2,5,8],[2,7,9],[2,4,7],[0,1,5],[0,6,9],[1,2,5],[1,4,6],[1,4,8],[1,4,8],[3,5,9],[3,7,8],[1,8,9],[2,7,8],[0,5,9],[0,8,9],[6,7,8],[3,7,9],[4,6,7],[4,5,8],[1,2,5],[0,1,6],[0,1,9],[0,7,8],[0,5,7],[1,2,8],[4,5,7],[0,3,5],[4,6,9],[0,4,6],[3,7,9],[1,2,7],[1,4,5],[1,2,6],[0,2,6],[1,2,7],[3,6,9],[1,5,8],[2,4,8],[3,6,9],[5,7,9],[6,7,9],[2,3,9],[1,4,6],[0,7,8],[0,2,8],[0,2,6],[0,7,8],[2,3,9],[2,4,9],[1,2,7],[0,6,9],[2,4,9],[5,7,8],[0,4,6],[3,4,8],[1,2,7],[1,3,7],[5,8,9],[1,2,5],[0,4,9],[0,7,9],[2,6,9],[3,5,9],[6,7,8],[2,3,5],[2,3,5],[3,4,7],[0,4,5],[1,2,8],[3,5,9],[0,1,9],[5,7,8],[0,1,7],[0,4,5],[1,2,8],[4,5,7],[5,7,8],[0,5,6],[2,5,6],[5,6,8],[0,1,5],[7,8,9],[0,3,5],[6,7,8],[0,1,2],[1,4,7],[5,7,9],[1,3,8],[2,3,6],[1,3,5],[0,1,2],[2,3,7],[3,5,7],[3,4,8],[2,4,8],[0,5,6],[1,3,8],[4,6,7],[1,3,4],[3,5,6],[2,7,8],[0,3,6],[2,6,7],[0,3,9],[2,6,8],[3,6,9],[1,8,9],[1,3,4],[2,4,6],[1,2,9],[0,2,7],[2,4,8],[5,6,8],[5,6,8],[1,4,8],[1,3,6],[1,3,4],[2,5,6],[5,6,8],[0,3,5],[0,5,8],[2,6,7],[3,6,7],[2,4,7],[1,3,4],[1,5,9],[3,5,6],[1,2,9],[3,4,6],[1,4,8],[4,7,8],[0,2,4],[0,1,3],[1,2,8],[0,3,7],[1,3,6],[1,4,5],[0,5,9],[0,2,5],[2,3,9],[2,3,6],[1,3,9],[3,7,8],[2,5,9],[1,5,8],[0,4,6],[0,3,7],[1,3,4],[1,2,3],[3,4,7],[0,5,8],[1,2,8],[3,4,5],[0,5,7],[0,3,4],[2,5,7],[2,3,4],[2,5,6],[0,4,8],[0,4,9],[0,2,5],[1,4,6],[2,6,8],[1,2,6],[2,5,6],[4,6,9],[3,4,9],[2,3,6],[1,3,5],[1,5,9],[1,3,7],[0,1,4],[4,5,7],[0,3,6],[1,3,8],[0,3,5],[0,4,6],[1,3,5],[6,7,8],[0,5,8],[4,5,6],[0,3,9],[0,2,7],[4,5,9],[0,8,9],[3,6,9],[1,2,7],[5,6,9],[5,7,8],[5,6,9],[3,4,9],[5,6,7],[0,7,8],[2,3,8],[3,4,9],[2,6,7],[0,2,4],[3,4,7],[1,3,7],[0,2,9],[2,3,7],[1,4,6],[5,6,8],[1,5,8],[0,4,7],[1,8,9],[3,5,7],[4,5,9],[4,6,8],[1,2,4],[0,6,7],[0,1,9],[2,4,5],[2,4,6],[3,6,7],[3,4,7],[0,2,6],[4,5,6],[0,2,5],[4,6,9],[6,7,8],[0,3,6],[1,5,7],[0,2,6],[6,7,9],[2,4,9],[1,2,5],[3,4,6],[3,4,5],[3,4,6],[0,2,7],[0,4,6],[2,8,9],[2,5,9],[0,5,8],[1,5,8],[0,4,8],[1,5,7],[1,3,4],[0,4,5],[1,2,4],[3,5,7],[5,6,7],[2,5,7],[3,5,9],[1,6,8],[0,3,8],[2,4,8],[1,3,5],[3,5,7],[1,7,9],[1,5,9],[3,4,7],[0,5,6],[1,4,6],[1,3,4],[2,3,8],[2,4,6],[1,6,9],[2,8,9],[0,2,4],[2,3,8],[1,5,9],[0,3,7],[2,3,5],[2,7,8],[3,5,9],[0,5,8],[1,7,9],[3,6,7],[6,7,9],[2,4,5],[1,7,9],[1,4,6],[1,6,7],[2,6,8],[2,6,9],[1,2,7],[3,5,7],[5,7,9],[2,4,7],[6,8,9],[2,4,5],[4,5,8],[0,1,6],[0,1,4],[0,1,3],[1,3,4],[0,2,3],[3,6,9],[6,8,9],[5,7,9],[1,4,7],[6,7,9],[2,3,5],[2,7,9],[2,8,9],[3,5,7],[1,7,8],[0,7,8],[0,1,2],[4,7,9],[3,4,8],[0,4,8],[3,8,9],[0,1,2],[0,5,6],[1,7,9],[1,3,4],[5,7,9],[0,8,9],[0,5,6],[1,2,6],[0,1,6],[1,4,6],[2,6,9],[0,3,7],[3,6,7],[0,3,8],[6,8,9],[0,3,5],[2,4,9],[0,5,7],[1,3,4],[1,4,9],[0,2,6],[0,2,8],[0,8,9],[2,7,8],[3,4,7],[2,5,8],[1,2,9],[1,5,6],[0,2,5],[5,6,8],[4,6,9],[0,2,4],[2,3,4],[2,5,6],[2,3,7],[1,5,8],[1,6,8],[5,6,8],[0,1,3],[4,7,8],[0,1,9],[1,2,9],[1,6,8],[0,2,6],[0,4,5],[1,8,9],[0,3,7],[2,8,9],[1,3,6],[0,5,8],[0,3,6],[0,1,2],[4,5,7],[0,4,9],[3,4,9],[2,3,9],[1,2,5],[2,7,9],[3,6,9],[0,2,4],[1,2,8],[0,2,3],[0,5,7],[0,3,8],[0,5,6],[3,6,8],[3,8,9],[2,6,7],[1,7,8],[5,8,9],[2,5,8],[1,5,8],[4,6,7],[5,6,7],[2,5,9],[0,1,9],[0,5,9],[1,3,4]],[[3,8,9],[4,5,6],[1,6,9],[0,1,7],[1,5,8],[4,5,6],[0,4,9],[0,2,4],[0,2,4],[4,6,7],[0,6,9],[0,1,2],[7,8,9],[3,6,7],[4,6,7],[6,8,9],[1,5,9],[2,3,6],[2,8,9],[2,6,9],[3,5,7],[0,2,9],[2,3,5],[0,4,8],[0,6,7],[4,5,6],[1,4,8],[7,8,9],[3,4,6],[5,6,8],[5,6,7],[6,7,8],[1,6,8],[2,3,7],[0,1,8],[1,6,9],[4,8,9],[5,7,8],[0,7,8],[2,3,8],[4,7,8],[6,7,9],[3,6,9],[2,3,5],[1,2,7],[3,7,9],[0,1,7],[3,6,9],[0,4,8],[3,6,9],[4,5,7],[2,4,9],[3,5,9],[1,6,8],[6,7,9],[2,3,8],[3,4,8],[3,5,6],[0,4,5],[2,7,9],[1,3,6],[6,7,8],[1,4,9],[0,5,6],[1,5,6],[0,3,8],[3,8,9],[2,4,5],[1,2,5],[1,3,8],[0,1,4],[1,2,7],[0,2,4],[4,5,7],[2,5,9],[3,5,7],[0,5,6],[0,1,3],[3,4,9],[2,3,4],[0,2,3],[0,6,7],[3,5,7],[3,7,8],[0,2,4],[3,8,9],[4,6,8],[1,7,9],[4,5,7],[0,4,7],[0,2,5],[0,8,9],[4,8,9],[3,7,8],[3,7,9],[1,2,5],[0,1,2],[1,2,9],[5,6,8],[3,4,6],[1,4,6],[0,3,9],[1,2,5],[3,4,8],[1,2,9],[2,7,8],[1,2,3],[1,7,9],[1,5,9],[4,5,9],[0,2,4],[0,1,7],[4,7,9],[0,2,7],[3,5,8],[0,1,9],[5,6,8],[0,6,9],[1,6,8],[2,4,7],[1,6,9],[5,7,9],[0,1,9],[7,8,9],[6,7,9],[0,3,4],[0,1,2],[0,3,9],[6,7,9],[2,3,7],[3,5,6],[0,1,7],[0,2,7],[2,7,8],[0,6,7],[0,7,9],[0,2,9],[0,2,5],[0,1,6],[1,2,9],[0,8,9],[4,5,8],[0,2,9],[5,6,9],[1,2,6],[1,7,8],[5,7,9],[0,5,8],[6,8,9],[2,6,7],[2,3,9],[4,7,8],[0,3,6],[0,2,5],[3,4,9],[4,5,6],[3,5,7],[0,3,9],[3,4,8],[0,3,8],[1,7,9],[1,4,7],[0,1,9],[5,6,8],[2,3,9],[1,3,9],[2,5,6],[4,8,9],[0,6,9],[1,4,8],[2,4,6],[1,2,9],[3,5,7],[2,6,7],[5,6,7],[2,4,9],[0,1,5],[6,8,9],[3,4,8],[1,7,9],[0,1,2],[0,1,9],[1,5,6],[1,2,4],[2,3,4],[2,3,8],[1,3,5],[1,3,7],[1,5,6],[1,4,8],[2,8,9],[1,2,4],[5,6,8],[3,5,8],[4,5,9],[1,2,7],[4,8,9],[4,7,8],[2,8,9],[4,7,9],[0,5,9],[1,4,9],[1,4,7],[0,2,6],[0,3,5],[0,5,7],[1,4,6],[0,4,8],[4,6,8],[1,3,4],[1,2,3],[2,3,5],[3,6,7],[1,7,8],[3,5,8],[2,3,6],[1,3,6],[2,5,7],[0,1,4],[4,8,9],[0,2,6],[2,4,8],[4,5,7],[2,6,7],[1,2,4],[0,1,3],[0,1,2],[0,4,7],[1,6,9],[3,4,5],[0,5,7],[6,7,8],[1,6,9],[3,4,9],[4,6,8],[1,2,9],[2,3,9],[4,6,9],[0,7,9],[0,5,9],[0,2,4],[1,7,8],[4,5,8],[3,5,6],[2,3,5],[0,2,4],[0,2,4],[5,7,9],[2,4,9],[4,8,9],[6,7,9],[1,5,8],[1,5,7],[0,7,9],[2,5,8],[2,4,6],[0,2,3],[0,7,8],[4,6,9],[2,3,4],[2,4,6],[2,3,4],[1,2,6],[2,3,9],[3,6,9],[5,6,9],[1,4,7],[2,6,9],[0,2,9],[1,2,4],[4,5,7],[2,7,8],[1,2,9],[3,8,9],[1,8,9],[0,5,7],[3,4,8],[0,5,7],[0,3,8],[2,4,8],[2,7,8],[1,5,6],[1,3,9],[0,4,6],[2,4,7],[2,3,5],[2,3,7],[0,6,7],[0,3,9],[3,4,8],[0,5,7],[1,4,9],[1,3,4],[1,3,7],[1,3,6],[4,5,8],[2,3,9],[5,8,9],[2,8,9],[0,5,6],[7,8,9],[1,2,9],[1,5,6],[3,5,7],[1,2,7],[0,1,3],[0,7,8],[2,6,8],[4,6,8],[0,1,7],[0,1,3],[0,1,7],[1,3,9],[2,4,6],[1,3,4],[1,4,5],[6,7,8],[1,5,7],[0,2,8],[0,2,4],[3,4,6],[7,8,9],[1,7,9],[0,3,9],[5,8,9],[0,6,7],[2,6,9],[4,6,8],[2,3,4],[0,4,8],[1,3,9],[0,2,5],[1,2,9],[5,6,9],[2,3,7],[1,4,5],[1,2,5],[1,4,7],[0,3,9],[1,2,8],[1,3,6],[1,4,6],[6,7,9],[0,3,9],[2,4,7],[0,5,9],[0,2,8],[0,1,6],[2,5,9],[4,6,9],[4,6,8],[2,4,7],[0,2,8],[4,6,7],[0,2,9],[4,5,7],[1,2,3],[2,3,7],[1,3,9],[1,2,4],[0,4,6],[0,4,5],[4,7,8],[1,5,8],[5,7,9],[3,4,5],[1,2,5],[1,6,7],[0,2,6],[3,4,5],[3,4,5],[4,8,9],[3,4,7],[3,4,8],[0,4,5],[0,7,8],[4,6,7],[4,8,9],[0,3,9],[3,7,8],[2,6,9],[3,6,7],[0,3,7],[5,8,9],[5,6,9],[1,5,8],[5,6,9],[1,5,6],[0,6,7],[1,3,7],[0,2,9],[2,5,6],[1,3,5],[7,8,9],[3,5,7],[0,7,9],[0,7,9],[3,5,9],[0,4,5],[6,7,9],[0,1,6],[0,1,9],[3,4,9],[1,5,7],[3,5,7],[1,6,8],[2,7,9],[5,7,8],[4,5,6],[4,5,8],[0,2,3],[0,2,6],[0,1,4],[0,6,8],[0,4,6],[1,7,9],[2,5,9],[0,2,7],[0,5,7],[0,3,5],[0,4,9],[0,8,9],[6,8,9],[0,4,9],[2,3,8],[2,4,8],[5,6,8],[4,5,9],[1,5,7],[2,3,7],[0,5,6],[1,3,8],[2,6,8],[0,2,3],[0,3,6],[1,3,8],[2,4,6],[5,7,8],[1,3,4],[4,5,7],[0,3,8],[2,3,8],[3,4,8],[3,6,9],[0,1,7],[2,5,6],[0,5,9],[2,6,9],[2,3,4],[1,4,5],[0,6,9],[0,1,7],[1,7,9],[2,6,8],[0,6,7],[0,1,9],[3,6,8],[2,4,8],[4,6,8],[4,5,8],[3,5,8],[2,6,9],[1,5,8],[1,5,7],[0,6,9],[5,7,8],[2,4,5],[1,2,7],[2,5,8],[6,7,9],[4,5,7],[2,4,5],[4,5,7],[4,5,8],[3,4,5],[6,8,9],[0,3,8],[1,7,9],[2,5,7],[1,2,8],[0,2,8],[4,6,8],[0,4,6],[2,3,6],[1,3,9],[0,5,8],[1,2,5],[4,8,9],[2,6,9],[4,5,9],[4,7,8],[2,6,8],[0,3,8],[0,7,9],[0,5,7],[2,3,4],[0,3,7],[2,3,5],[3,5,9],[5,7,8],[0,4,7],[1,2,7],[0,4,5],[1,3,4],[0,4,9],[2,3,9],[2,3,6],[0,4,5],[0,2,5],[5,7,9],[1,4,7],[0,1,5]],[[3,4,8],[1,8,9],[0,5,7],[3,5,6],[1,3,4],[3,6,7],[3,8,9],[4,6,7],[2,4,6],[0,5,8],[3,6,8],[2,6,8],[2,7,8],[1,8,9],[3,5,7],[2,5,8],[2,5,6],[2,3,6],[0,3,8],[0,2,6],[0,2,7],[1,2,6],[3,4,7],[0,2,6],[2,7,9],[4,5,6],[0,2,4],[2,3,7],[5,7,8],[0,1,8],[4,6,7],[7,8,9],[0,4,9],[2,7,9],[0,8,9],[2,5,6],[0,1,4],[0,1,7],[0,2,8],[6,7,9],[0,1,9],[5,8,9],[7,8,9],[0,1,8],[4,5,9],[1,4,6],[1,8,9],[2,3,9],[0,3,4],[0,3,8],[3,8,9],[0,4,6],[2,5,6],[1,6,8],[0,3,6],[1,2,9],[1,4,5],[0,7,8],[1,6,7],[3,4,9],[1,3,6],[3,5,8],[0,1,7],[0,3,7],[0,1,5],[0,3,9],[0,4,5],[2,3,6],[1,2,7],[1,5,8],[1,3,5],[0,1,3],[1,5,9],[1,4,7],[3,4,6],[0,2,5],[5,8,9],[3,4,6],[6,8,9],[0,8,9],[6,7,8],[1,6,9],[1,2,8],[0,1,7],[4,5,8],[3,5,9],[0,6,8],[0,6,9],[3,5,8],[5,7,8],[5,8,9],[2,5,6],[1,2,8],[0,2,5],[1,5,9],[2,5,8],[6,8,9],[1,4,6],[1,5,7],[1,2,7],[6,8,9],[4,6,8],[4,5,7],[2,4,9],[0,3,4],[4,8,9],[2,3,4],[4,5,9],[3,7,8],[1,5,8],[0,5,8],[5,6,8],[0,3,6],[0,5,9],[1,6,8],[1,4,5],[1,5,7],[0,2,4],[1,2,3],[1,4,8],[0,4,8],[0,5,7],[0,1,8],[0,4,7],[3,6,9],[1,4,9],[0,2,3],[0,1,6],[1,2,3],[3,7,8],[6,8,9],[0,3,9],[1,2,8],[0,3,4],[0,5,6],[0,6,8],[0,1,8],[1,5,6],[1,6,7],[1,2,3],[2,4,7],[1,3,5],[0,5,9],[0,7,9],[4,6,8],[4,6,9],[1,7,9],[3,4,7],[1,6,9],[5,6,8],[2,6,8],[3,7,9],[0,4,6],[1,5,8],[2,4,9],[0,8,9],[1,4,8],[0,6,7],[0,2,4],[1,5,6],[0,3,9],[0,4,5],[4,5,8],[5,7,9],[0,3,9],[2,4,7],[0,6,8],[0,2,3],[2,3,4],[1,2,7],[5,7,8],[1,5,9],[1,2,8],[0,5,9],[5,7,9],[4,6,7],[1,4,7],[0,4,6],[0,4,5],[2,3,9],[2,8,9],[4,6,8],[1,2,5],[3,7,9],[1,2,4],[1,6,7],[0,4,9],[0,5,7],[2,3,7],[2,6,9],[0,2,3],[5,6,9],[4,6,9],[0,4,8],[0,1,7],[1,6,9],[1,3,4],[5,6,7],[4,6,8],[0,1,5],[2,8,9],[2,6,8],[0,1,4],[2,5,8],[2,4,5],[1,3,5],[2,3,4],[6,8,9],[0,2,3],[0,7,8],[6,7,9],[1,2,6],[1,8,9],[0,3,9],[6,7,9],[0,2,6],[2,7,9],[0,1,6],[2,7,9],[0,1,3],[4,7,9],[1,5,7],[2,3,8],[5,7,9],[4,8,9],[0,1,4],[0,5,8],[1,5,7],[0,3,9],[0,1,9],[5,6,7],[0,5,9],[1,2,3],[4,5,6],[0,7,8],[0,2,9],[0,3,6],[0,2,6],[0,6,8],[0,5,7],[3,7,8],[0,1,8],[2,3,4],[1,6,8],[2,5,9],[3,6,8],[2,4,5],[7,8,9],[0,5,9],[5,6,9],[6,7,9],[1,8,9],[2,4,6],[3,4,6],[2,3,4],[0,1,7],[2,6,9],[5,6,9],[1,6,8],[1,6,7],[0,2,8],[0,2,4],[3,5,9],[0,1,5],[3,4,8],[4,6,7],[0,1,9],[0,3,8],[1,3,6],[1,2,8],[1,4,7],[4,6,9],[3,6,9],[0,1,2],[0,2,9],[0,4,6],[1,5,9],[3,4,7],[5,8,9],[2,5,9],[1,3,9],[0,4,9],[2,8,9],[2,5,6],[0,4,8],[3,5,9],[2,7,9],[3,8,9],[0,1,9],[4,8,9],[3,7,8],[0,1,7],[4,7,8],[2,5,9],[0,2,6],[2,3,9],[3,5,7],[1,5,8],[3,8,9],[0,4,6],[2,4,7],[2,3,6],[1,2,6],[0,5,8],[3,5,8],[3,4,5],[3,5,9],[2,3,6],[4,7,9],[1,2,4],[0,6,9],[2,3,6],[0,3,9],[1,6,9],[3,6,7],[2,5,8],[5,6,8],[3,4,7],[0,6,9],[4,5,7],[1,2,9],[1,2,6],[0,5,8],[2,5,9],[1,2,5],[3,4,6],[7,8,9],[0,1,6],[2,4,7],[1,2,5],[0,4,7],[2,5,9],[4,5,8],[1,8,9],[0,2,4],[2,5,6],[3,5,8],[3,5,8],[2,3,5],[3,4,7],[4,7,8],[3,8,9],[1,3,5],[1,6,7],[1,4,9],[0,1,9],[0,1,8],[7,8,9],[5,8,9],[1,4,7],[3,5,9],[0,1,7],[3,4,5],[1,3,5],[4,5,8],[1,5,8],[1,3,6],[3,7,9],[1,4,9],[3,4,5],[3,4,5],[5,7,8],[1,5,8],[2,7,8],[3,6,7],[4,6,9],[0,1,5],[6,8,9],[0,2,8],[0,2,7],[0,3,6],[2,6,8],[2,6,7],[2,6,8],[5,7,9],[0,5,9],[0,2,4],[0,5,6],[3,4,8],[4,6,7],[2,5,7],[1,2,8],[0,3,4],[4,5,7],[2,4,9],[7,8,9],[0,2,5],[2,5,9],[1,6,9],[4,5,8],[4,7,9],[3,6,9],[1,4,8],[1,5,6],[2,6,7],[3,4,7],[0,3,7],[1,4,5],[7,8,9],[0,5,7],[5,6,9],[5,8,9],[3,5,7],[5,7,8],[0,2,8],[4,6,9],[4,6,7],[0,6,8],[0,4,5],[0,1,4],[4,6,7],[2,5,9],[2,3,4],[4,5,8],[5,7,9],[0,6,8],[2,3,9],[2,3,5],[5,7,9],[2,4,8],[3,5,7],[2,3,9],[0,2,7],[2,6,7],[4,7,9],[2,5,9],[0,5,7],[5,6,7],[0,7,8],[0,2,7],[6,7,8],[0,8,9],[1,4,8],[1,4,7],[7,8,9],[3,6,7],[1,2,6],[1,4,8],[4,7,8],[1,5,7],[5,8,9],[2,4,5],[1,3,5],[4,6,9],[0,2,6],[0,1,7],[1,2,4],[4,5,7],[2,6,8],[5,7,9],[3,4,7],[0,1,5],[1,2,5],[1,7,8],[4,7,9],[0,4,6],[1,4,6],[0,7,8],[2,4,5],[2,3,4],[6,8,9],[1,4,8],[1,2,9],[0,3,6],[1,5,9],[2,5,7],[5,7,8],[2,6,9],[1,2,8],[3,6,9],[0,2,6],[0,4,5],[4,5,8],[2,7,8],[0,3,7],[0,4,8],[1,6,8],[2,5,7],[1,5,9],[0,1,2],[3,6,9],[2,7,8],[0,2,7],[0,2,3],[1,8,9],[0,3,6],[2,4,6],[2,3,6],[5,7,9],[1,4,5],[1,5,8],[0,3,5],[0,1,4],[0,4,8],[0,4,7],[2,3,7],[3,4,5],[0,3,7],[1,2,8],[1,3,5],[0,4,9],[2,3,4],[0,1,6],[2,4,8],[0,4,6],[0,1,8],[4,6,7],[0,7,8],[2,5,8],[3,6,9],[3,6,9],[0,8,9]]]
def setup_inputs(rng):
    return {"x": rng.standard_normal((N, 128, TOK), dtype=np.float32).astype(ml_dtypes.bfloat16), "gate": (0.5 * rng.integers(1, 4, size=(N, K, TOK)) * (2 * rng.integers(0, 2, size=(N, K, TOK)) - 1)).astype(np.float32).astype(ml_dtypes.bfloat16), "w1": (rng.standard_normal((N, 128, FT * 128), dtype=np.float32) / 8).astype(ml_dtypes.bfloat16), "w2": (rng.standard_normal((N, 128, FT * 128), dtype=np.float32) / 8).astype(ml_dtypes.bfloat16)}
def setup_inputs_big(rng):
    d = setup_inputs(rng)
    for k in ("x", "gate", "w1", "w2"): d[k] = (d[k].astype(np.float32) * 1024.0).astype(d[k].dtype)
    return d
def setup_inputs_small(rng):
    d = setup_inputs(rng)
    for k in ("x", "gate", "w1", "w2"): d[k] = (d[k].astype(np.float32) * (1 / 1024.0)).astype(d[k].dtype)
    return d
def reference(x, gate, w1, w2):
    X, GATE, W1, W2 = x.astype(np.float64), gate.astype(np.float64), w1.astype(np.float64), w2.astype(np.float64)
    y = np.zeros((N, 128, TOK))
    for r in range(N):
        for t in range(TOK):
            for i, e in enumerate(ROUTE[r][t]):
                hid = np.maximum(W1[e].T @ X[r][:, t], 0.0)
                y[r][:, t] += GATE[r][i, t] * sum(W2[e][:, 128 * f:128 * f + 128].T @ hid[128 * f:128 * f + 128] for f in range(FT))
    return {"y": y.astype(ml_dtypes.bfloat16)}

@@ -1,0 +1,390 @@
+from concourse.bass import DstId, RemoteDMATransfer
+from concourse.mybir import AluOpType
+
+NSIM = 256
+NH = 2
+N0 = 4
+NREL = 2
+NIDLE = 1
+WENG = 4
+PENG = 16
+NCMAX = 32
+BIG, TINY, MAGIC = 2.0 ** 25, 2.0 ** -25, 1.5 * 2.0 ** 23
+
+SCRATCH = {
+    "xg": ("sbuf", [128, 524], "bfloat16"),
+    "wt": ("sbuf", [128, 2560], "bfloat16"),
+    "wr": ("sbuf", [128, 256], "bfloat16"),
+    "rl": ("sbuf", [128, 5120], "bfloat16"),
+    "sg": ("sbuf", [128, 5120], "bfloat16"),
+    "zer": ("sbuf", [128, 512], "bfloat16"),
+    "fb": ("sbuf", [128, 128], "bfloat16"),
+    "gm": ("sbuf", [128, 512], "bfloat16"),
+    "sel": ("sbuf", [128, 1280], "bfloat16"),
+    "grow": ("sbuf", [1, 1536], "bfloat16"),
+    "ap": ("sbuf", [1, 155], "bfloat16"),
+    "ip": ("sbuf", [1, 226], "bfloat16"),
+    "one": ("sbuf", [1, 128], "bfloat16"),
+    "lr": ("sbuf", [1, 152], "float32"),
+    "lb": ("sbuf", [1, 152], "float32"),
+    "lp": ("sbuf", [1, 152], "float32"),
+    "rw": ("sbuf", [1, 5 * NCMAX], "float32"),
+    "mag": ("sbuf", [128, NCMAX], "float32"),
+    "tin": ("sbuf", [128, NCMAX], "float32"),
+    "zf": ("sbuf", [128, NCMAX], "float32"),
+    "a1": ("sbuf", [128, NCMAX], "float32"),
+    "a2": ("sbuf", [128, NCMAX], "float32"),
+    "a3": ("sbuf", [128, NCMAX], "float32"),
+    "a4": ("sbuf", [128, NCMAX], "float32"),
+    "fo": ("sbuf", [128, NCMAX], "bfloat16"),
+    "part": ("sbuf", [128, 512 * max(NH, 1)], "bfloat16"),
+    "ids": ("sbuf", [128, 129], "bfloat16"),
+    "idd": ("dram", [129, 128], "bfloat16"),
+    "ident": ("sbuf", [128, 128], "bfloat16"),
+    "yo": ("sbuf", [128, 512], "bfloat16"),
+    "ph0": ("psum", [128, 512], "float32"), "ph1": ("psum", [128, 512], "float32"), "ph2": ("psum", [128, 512], "float32"),
+    "pg0": ("psum", [128, 512], "float32"), "pg1": ("psum", [128, 512], "float32"), "pg2": ("psum", [128, 512], "float32"),
+    "py": ("psum", [128, 512], "float32"), "pgl": ("psum", [128, 512], "float32"),
+}
+SEMAPHORES = (["cs", "se", "sv", "gl", "ldx", "ldw", "ldg", "xa", "wrs", "fa", "gms", "m2", "ev", "st", "loc", "hp", "hv",
+               "i1", "i2"]
+              + ["w%d" % e for e in range(10)] + ["pa%d" % h for h in range(max(NH, 1))]
+              + ["%s_%d" % (s, k) for s in ("m1", "rl", "gb", "mu") for k in range(10)])
+
+_CACHE = {}
+
+
+def _pick(mask, n):
+    b = [i for i in range(32) if (mask >> i) & 1][:n]
+    return sum(1 << i for i in b)
+
+
+def _ids(topo, dsts, src):
+    out = []
+    for d in dsts:
+        rid, pid = topo.addr(d, src)
+        out.append(DstId(rid=rid, pnc=pid))
+    return out
+
+
+def _word(route, k, c):
+    bits = 0
+    for b in range(4):
+        for x in range(2):
+            for i in range(3):
+                if route[128 * b + c][i] == 2 * k + x:
+                    bits |= 1 << (6 * b + 3 * x + i)
+    full = (1 << 23) - 1
+    low = bits & full
+    if bits >> 23:
+        return -float(1 + 2 * (full ^ low))
+    return float(1 + 2 * low)
+
+
+def _plan(T, topo):
+    if "p" in _CACHE:
+        return _CACHE["p"]
+    cores = list(T.cores)
+    n = len(cores)
+
+    def key(c):
+        return (topo.host(c), topo.chip(c))
+    bychip = {}
+    for c in range(NSIM):
+        bychip.setdefault(key(c), []).append(c)
+    rankkeys = [key(c) for c in cores]
+    idle = [k for k in sorted(bychip) if k not in rankkeys]
+    used = []
+    role = {}
+    P = {"cores": cores, "role": role, "comp": [], "relays": [], "wh": [], "same": [], "cross": [], "lists": {}}
+    arr = [[None] * n for _ in range(n)]
+    for r, R in enumerate(cores):
+        mine = [c for c in bychip[key(R)] if c != R]
+        same = [d for d in range(n) if d != r and topo.may_write(R, cores[d])]
+        cross = [d for d in range(n) if d != r and not topo.may_write(R, cores[d])]
+        ports = [c for c in mine if all(topo.may_write(c, cores[d]) for d in cross)]
+        far = [c for c in ports if topo.die(c) != topo.die(R)]
+        relays = (far or ports)[:NREL]
+        comp = [c for c in mine if c not in relays and topo.die(c) == topo.die(R)][:NH]
+        wh = [c for c in mine if c not in relays and c not in comp]
+        got = 0
+        for k in idle:
+            if got < NIDLE and k not in used and topo.same_plane(bychip[k][0], R):
+                used.append(k)
+                got += 1
+                wh += [c for c in bychip[k] if topo.may_write(c, R)]
+        same.sort(key=lambda d: (d - r) % n)
+        cross.sort(key=lambda d: (d - r) % n)
+        arr[r][r] = (0, 0)
+        for pos, d in enumerate(same):
+            arr[d][r] = (1, pos)
+        split = [cross[j::len(relays)] for j in range(len(relays))]
+        for part in split:
+            for pos, d in enumerate(part):
+                arr[d][r] = (2, pos)
+        role[R] = ("rank", r, 0)
+        for h, c in enumerate(comp):
+            role[c] = ("comp", r, h)
+        for j, c in enumerate(relays):
+            role[c] = ("relay", r, j)
+        for i, c in enumerate(wh):
+            role[c] = ("word", r, i)
+        P["comp"].append(comp)
+        P["relays"].append(relays)
+        P["wh"].append(wh)
+        P["same"].append(same)
+        P["cross"].append(split)
+    owner = [[None] * n for _ in range(n)]
+    for d, R in enumerate(cores):
+        order = sorted(range(n), key=lambda e: arr[d][e])
+        others = order[1:]
+        comp = P["comp"][d]
+        keep = (N0 - 1) if comp else len(others)
+        cut = len(others) - keep
+        lists = {R: [order[0]] + others[cut:]}
+        for h, c in enumerate(comp):
+            lists[c] = others[:cut][h::len(comp)]
+        for c in lists:
+            P["lists"][c] = [(e, arr[d][e][0]) for e in lists[c]]
+            for e in lists[c]:
+                owner[d][e] = c
+    P["owner"] = owner
+    _CACHE["p"] = P
+    return P
+
+
+def _relay(g, core, T, topo, P, r, j):
+    dsts = [P["owner"][d][r] for d in P["cross"][r][j]]
+    if not dsts:
+        return
+    m = _pick(topo.mask(core, dsts[0]), 8)
+    g.wait_ge(T.sem.wrs, 8)
+    g.remote_dma_fused([RemoteDMATransfer(dst_ids=_ids(topo, dsts, core), dma_engine_mask=m, remote_sem=T.sem["w%d" % r],
+                                          srcs=[T.wr[:, :]], dsts=[T.wt[:, r * 256:r * 256 + 256]] * len(dsts))],
+                       local_sem=T.sem.loc)
+    g.wait_ge(T.sem.loc, 8)
+
+
+def _words(g, core, T, topo, P, r, i):
+    sem, V, PE = T.sem, g.vector, g.tensor
+    nw = len(P["wh"][r])
+    c0, c1 = i * 128 // nw, (i + 1) * 128 // nw
+    nc = c1 - c0
+    route = T.tables["ROUTE"][r]
+    cnt = [0]
+
+    def fill(ap, v):
+        V.memset(ap, v).then_inc(sem.cs, 1)
+        cnt[0] += 1
+    fill(T.lr[:, :], 0.0)
+    fill(T.lb[0:1, 0:56], 1.0)
+    for b in range(1, 4):
+        fill(T.lb[0:1, 24 + 32 * b:56 + 32 * b], 2.0 ** (-6 * b))
+    fill(T.mag[:, 0:nc], MAGIC)
+    fill(T.tin[:, 0:nc], TINY)
+    fill(T.zf[:, 0:nc], 0.0)
+    V.wait_ge(sem.cs, cnt[0])
+    for q in range(6):
+        fill(T.lr[0:1, 24 + q:152:32], 2.0 ** (-(q + 2)))
+    V.wait_ge(sem.cs, cnt[0])
+    V.tensor_tensor(T.lp[:, :], T.lr[:, :], T.lb[:, :], AluOpType.mult).then_inc(sem.cs, 1)
+    cnt[0] += 1
+    for k in range(5):
+        for c in range(nc):
+            fill(T.rw[0:1, k * nc + c:k * nc + c + 1], _word(route, k, c0 + c))
+    PE.wait_ge(sem.cs, cnt[0])
+    u = T.ph0[:, 0:nc]
+    for k in range(5):
+        PE.matmul(u, T.lp[0:1, 24 - 6 * k:152 - 6 * k], T.rw[0:1, k * nc:(k + 1) * nc], k == 0, k == 4).then_inc(sem.hp, 1)
+    V.wait_ge(sem.cs, cnt[0])
+    V.wait_ge(sem.hp, 5)
+    steps = [(T.a1, u, T.mag, AluOpType.add), (T.a2, T.a1, T.mag, AluOpType.subtract), (T.a3, T.a2, u, AluOpType.subtract),
+             (T.a4, T.a3, T.tin, AluOpType.min), (T.fo, T.a4, T.zf, AluOpType.max)]
+    for s, (o, a, b, op) in enumerate(steps):
+        a = a if a is u else a[:, 0:nc]
+        b = b if b is u else b[:, 0:nc]
+        V.tensor_tensor(o[:, 0:nc], a, b, op).then_inc(sem.hv, 1)
+        if s < 4:
+            V.wait_ge(sem.hv, s + 1)
+    dsts = [P["cores"][r]] + P["comp"][r]
+    m = _pick(topo.mask(core, dsts[0]), WENG)
+    g.wait_ge(sem.hv, 5)
+    g.remote_dma_fused([RemoteDMATransfer(dst_ids=_ids(topo, dsts, core), dma_engine_mask=m, remote_sem=sem.fa,
+                                          srcs=[T.fo[:, 0:nc]], dsts=[T.fb[:, c0:c1]] * len(dsts))], local_sem=sem.loc)
+    g.wait_ge(sem.loc, WENG)
+
+
+def _compute(g, core, T, topo, P, r, h):
+    sem, V, PE, S, A = T.sem, g.vector, g.tensor, g.sync, g.scalar
+    R = P["cores"][r]
+    is_rank = core == R
+    L = P["lists"][core]
+    n = len(L)
+    n1 = len([1 for e, hp in L if hp <= 1])
+    comp = P["comp"][r]
+    nh = len(comp)
+    ph, pg = [T.ph0, T.ph1, T.ph2], [T.pg0, T.pg1, T.pg2]
+    o = r * 256
+    nx = 32 if nh else 16
+    if is_rank:
+        S.dma_start(T.wt[:, o:o + 128], T.w1[:, :]).then_inc(sem.ldw, 16)
+        A.dma_start(T.wt[:, o + 128:o + 256], T.w2[:, :]).then_inc(sem.ldw, 16)
+        S.dma_start(T.xg[:, 0:512], T.x[:, :]).then_inc(sem.ldx, 16)
+        A.dma_start(T.grow[:, :], T.gate[:, :]).then_inc(sem.ldg, 16)
+        if nh:
+            A.dma_start(T.xg[:, 512:524], T.gate[:, :]).then_inc(sem.ldx, 16)
+    else:
+        S.wait_ge(sem.xa, 8)
+        S.dma_start(T.grow[:, :], T.xg[:, 512:524]).then_inc(sem.ldg, 16)
+    loc = 0
+    if is_rank:
+        src = T.wt[:, o:o + 256]
+        sd = [P["owner"][d][r] for d in P["same"][r]]
+        rel = P["relays"][r]
+        off = _pick(topo.mask(R, sd[0]), 8)
+        on = _pick(topo.mask(R, rel[0]) & ~off, 8)
+        g.wait_ge(sem.ldw, 32)
+        g.remote_dma_fused([
+            RemoteDMATransfer(dst_ids=_ids(topo, rel, R), dma_engine_mask=on, remote_sem=sem.wrs,
+                              srcs=[src], dsts=[T.wr[:, :]] * len(rel)),
+            RemoteDMATransfer(dst_ids=_ids(topo, sd, R), dma_engine_mask=off, remote_sem=sem["w%d" % r],
+                              srcs=[src], dsts=[src] * len(sd))], local_sem=sem.loc)
+        loc += 16
+        if nh:
+            g.wait_ge(sem.ldx, nx)
+            g.remote_dma_fused([RemoteDMATransfer(dst_ids=_ids(topo, comp, R), dma_engine_mask=on, remote_sem=sem.xa,
+                                                  srcs=[T.xg[:, :]], dsts=[T.xg[:, :]] * nh)], local_sem=sem.loc)
+            loc += 8
+    cnt = [0]
+
+    def fill(ap, v):
+        V.memset(ap, v).then_inc(sem.cs, 1)
+        cnt[0] += 1
+    fill(T.ap[:, :], 0.0)
+    fill(T.ip[:, :], 0.0)
+    fill(T.one[:, :], BIG)
+    fill(T.zer[:, :], 0.0)
+    if is_rank and nh:
+        fill(T.ids[:, :], 0.0)
+    V.wait_ge(sem.cs, cnt[0])
+    for b in range(4):
+        fill(T.ap[0:1, 27 + 32 * b:30 + 32 * b], 1.0)
+    fill(T.ip[0:1, 98:126:3], 1.0)
+    if is_rank and nh:
+        fill(T.ids[:, 0:1], 1.0)
+    ncs = cnt[0]
+    V.wait_ge(sem.cs, ncs)
+    if is_rank and nh:
+        S.wait_ge(sem.cs, ncs)
+        S.dma_start(T.idd[:, :], T.ids[:, :]).then_inc(sem.i1, 16)
+        S.wait_ge(sem.i1, 16)
+        S.dma_start(T.ident[:, :], T.idd[0:128, :]).then_inc(sem.i2, 16)
+    PE.wait_ge(sem.cs, ncs)
+    for k, (e, hp) in enumerate(L):
+        PE.matmul(ph[k // 4][:, (k % 4) * 128:(k % 4) * 128 + 128], T.ap[0:1, 27 - 3 * e:155 - 3 * e], T.one[0:1, :],
+                  True, True).then_inc(sem.se, 1)
+    V.wait_ge(sem.se, n)
+    nb = (n + 3) // 4
+    for b in range(nb):
+        w = min(4, n - 4 * b) * 128
+        V.tensor_copy(T.sel[:, b * 512:b * 512 + w], ph[b][:, 0:w]).then_inc(sem.sv, 1)
+    PE.wait_ge(sem.ldg, 16)
+    for b in range(4):
+        for i in range(3):
+            PE.matmul(T.pgl[:, 128 * b:128 * b + 128], T.ip[0:1, 98 - 32 * b - i:226 - 32 * b - i],
+                      T.grow[0:1, 512 * i + 128 * b:512 * i + 128 * b + 128], i == 0, i == 2).then_inc(sem.gl, 1)
+    tot = n + (nh if is_rank else 0)
+    done = [0]
+
+    def acc(lhsT, rhs):
+        PE.matmul(T.py[:, :], lhsT, rhs, done[0] == 0, done[0] == tot - 1).then_inc(sem.m2, 1)
+        done[0] += 1
+
+    def mm1(k):
+        e, hp = L[k]
+        if hp == 0:
+            PE.wait_ge(sem.ldw, 32)
+        else:
+            PE.wait_ge(sem["w%d" % e], 8)
+        if k >= 3:
+            PE.wait_ge(sem["rl_%d" % (k - 3)], 1)
+        PE.matmul(ph[k % 3][:, :], T.wt[:, e * 256:e * 256 + 128], T.xg[:, 0:512], True, True).then_inc(sem["m1_%d" % k], 1)
+
+    def gb(k):
+        if k >= 3:
+            PE.wait_ge(sem["mu_%d" % (k - 3)], 1)
+        PE.matmul(pg[k % 3][:, :], T.sel[:, k * 128:k * 128 + 128], T.gm[:, :], True, True).then_inc(sem["gb_%d" % k], 1)
+
+    def mm2(k):
+        e = L[k][0]
+        PE.wait_ge(sem["mu_%d" % k], 1)
+        acc(T.wt[:, e * 256 + 128:e * 256 + 256], T.sg[:, k * 512:k * 512 + 512])
+
+    def relu(k):
+        V.wait_ge(sem["m1_%d" % k], 1)
+        V.tensor_tensor(T.rl[:, k * 512:k * 512 + 512], ph[k % 3][:, :], T.zer[:, :], AluOpType.max).then_inc(sem["rl_%d" % k], 1)
+
+    def mult(k):
+        V.wait_ge(sem["gb_%d" % k], 1)
+        V.wait_ge(sem["rl_%d" % k], 1)
+        V.tensor_tensor(T.sg[:, k * 512:k * 512 + 512], T.rl[:, k * 512:k * 512 + 512], pg[k % 3][:, :],
+                        AluOpType.mult).then_inc(sem["mu_%d" % k], 1)
+
+    if is_rank:
+        PE.wait_ge(sem.ldx, nx)
+    else:
+        PE.wait_ge(sem.xa, 8)
+    PE.wait_ge(sem.sv, nb)
+    for k in range(n1):
+        mm1(k)
+    PE.wait_ge(sem.gms, 4)
+    for k in range(n):
+        if k >= n1:
+            mm1(k)
+        gb(k)
+        if k >= 1:
+            mm2(k - 1)
+    mm2(n - 1)
+    if is_rank and nh:
+        PE.wait_ge(sem.i2, 16)
+        for j in range(nh):
+            PE.wait_ge(sem["pa%d" % j], PENG)
+            acc(T.ident[:, :], T.part[:, j * 512:j * 512 + 512])
+
+    for k in range(n1):
+        relu(k)
+    V.wait_ge(sem.fa, WENG * len(P["wh"][r]))
+    V.wait_ge(sem.gl, 12)
+    for b in range(4):
+        V.tensor_tensor(T.gm[:, 128 * b:128 * b + 128], T.fb[:, :], T.pgl[:, 128 * b:128 * b + 128],
+                        AluOpType.mult).then_inc(sem.gms, 1)
+    for k in range(n):
+        if k >= n1:
+            relu(k)
+        mult(k)
+    V.wait_ge(sem.m2, tot)
+    V.tensor_copy(T.yo[:, :], T.py[:, :]).then_inc(sem.ev, 1)
+    if is_rank:
+        S.wait_ge(sem.ev, 1)
+        S.dma_start(T.y[:, :], T.yo[:, :]).then_inc(sem.st, 16)
+        S.wait_ge(sem.st, 16)
+    else:
+        rid, pid = topo.addr(R, core)
+        g.wait_ge(sem.ev, 1)
+        g.remote_dma(T.part[:, h * 512:h * 512 + 512], T.yo[:, :], sem["pa%d" % h], sem.loc, pid, rid,
+                     _pick(topo.mask(core, R), PENG))
+        loc += PENG
+    g.wait_ge(sem.loc, loc)
+
+
+def rank_program(g, core, T, topo):
+    P = _plan(T, topo)
+    if core not in P["role"]:
+        return
+    kind, r, i = P["role"][core]
+    if kind == "relay":
+        _relay(g, core, T, topo, P, r, i)
+    elif kind == "word":
+        _words(g, core, T, topo, P, r, i)
+    else:
+        _compute(g, core, T, topo, P, r, i)

@@ -3,12 +3,12 @@ from concourse.mybir import AluOpType
 
 NSIM = 256
 NH = 2
-N0 = 4
+N0 = 6
 NREL = 2
-NIDLE = 1
-WENG = 4
+NIDLE = 13
+WENG = 8
 PENG = 16
-NCMAX = 32
+NCMAX = 8
 BIG, TINY, MAGIC = 2.0 ** 25, 2.0 ** -25, 1.5 * 2.0 ** 23
 
 SCRATCH = {
@@ -46,8 +46,8 @@ SCRATCH = {
     "pg0": ("psum", [128, 512], "float32"), "pg1": ("psum", [128, 512], "float32"), "pg2": ("psum", [128, 512], "float32"),
     "py": ("psum", [128, 512], "float32"), "pgl": ("psum", [128, 512], "float32"),
 }
-SEMAPHORES = (["cs", "se", "sv", "gl", "ldx", "ldw", "ldg", "xa", "wrs", "fa", "gms", "m2", "ev", "st", "loc", "hp", "hv",
-               "i1", "i2"]
+SEMAPHORES = (["cs", "wc", "se", "sv", "gl", "ldx", "ldw", "ldg", "xa", "wrs", "fa", "gms", "m2", "ev0", "ev1", "st", "loc",
+               "hp", "hv", "i1", "i2"]
               + ["w%d" % e for e in range(10)] + ["pa%d" % h for h in range(max(NH, 1))]
               + ["%s_%d" % (s, k) for s in ("m1", "rl", "gb", "mu") for k in range(10)])
 
@@ -93,10 +93,10 @@ def _plan(T, topo):
     for c in range(NSIM):
         bychip.setdefault(key(c), []).append(c)
     rankkeys = [key(c) for c in cores]
-    idle = [k for k in sorted(bychip) if k not in rankkeys]
-    used = []
+    idle = [c for k in sorted(bychip) if k not in rankkeys for c in bychip[k]]
+    used = {}
     role = {}
-    P = {"cores": cores, "role": role, "comp": [], "relays": [], "wh": [], "same": [], "cross": [], "lists": {}}
+    P = {"cores": cores, "role": role, "comp": [], "relays": [], "wh": [], "same": [], "cross": [], "lists": {}, "cols": {}}
     arr = [[None] * n for _ in range(n)]
     for r, R in enumerate(cores):
         mine = [c for c in bychip[key(R)] if c != R]
@@ -106,32 +106,40 @@ def _plan(T, topo):
         far = [c for c in ports if topo.die(c) != topo.die(R)]
         relays = (far or ports)[:NREL]
         comp = [c for c in mine if c not in relays and topo.die(c) == topo.die(R)][:NH]
-        wh = [c for c in mine if c not in relays and c not in comp]
-        got = 0
-        for k in idle:
-            if got < NIDLE and k not in used and topo.same_plane(bychip[k][0], R):
-                used.append(k)
-                got += 1
-                wh += [c for c in bychip[k] if topo.may_write(c, R)]
+        rest = [c for c in mine if c not in relays and c not in comp]
+        onchip = len(rest)
+        for c in idle:
+            if len(rest) < onchip + NIDLE and c not in used and topo.same_plane(c, R) and topo.may_write(c, R):
+                used[c] = 1
+                rest.append(c)
+        pos = 0
+        for c in comp:
+            P["cols"][c] = (pos, pos + 8)
+            pos += 8
+        for c in relays:
+            P["cols"][c] = (pos, pos + 2)
+            pos += 2
+        for i, c in enumerate(rest):
+            P["cols"][c] = (pos + i * (128 - pos) // len(rest), pos + (i + 1) * (128 - pos) // len(rest))
         same.sort(key=lambda d: (d - r) % n)
         cross.sort(key=lambda d: (d - r) % n)
         arr[r][r] = (0, 0)
-        for pos, d in enumerate(same):
-            arr[d][r] = (1, pos)
+        for p_, d in enumerate(same):
+            arr[d][r] = (1, p_)
         split = [cross[j::len(relays)] for j in range(len(relays))]
         for part in split:
-            for pos, d in enumerate(part):
-                arr[d][r] = (2, pos)
+            for p_, d in enumerate(part):
+                arr[d][r] = (2, p_)
+        for c in rest:
+            role[c] = ("word", r, 0)
         role[R] = ("rank", r, 0)
         for h, c in enumerate(comp):
             role[c] = ("comp", r, h)
         for j, c in enumerate(relays):
             role[c] = ("relay", r, j)
-        for i, c in enumerate(wh):
-            role[c] = ("word", r, i)
         P["comp"].append(comp)
         P["relays"].append(relays)
-        P["wh"].append(wh)
+        P["wh"].append(comp + relays + rest)
         P["same"].append(same)
         P["cross"].append(split)
     owner = [[None] * n for _ in range(n)]
@@ -139,8 +147,7 @@ def _plan(T, topo):
         order = sorted(range(n), key=lambda e: arr[d][e])
         others = order[1:]
         comp = P["comp"][d]
-        keep = (N0 - 1) if comp else len(others)
-        cut = len(others) - keep
+        cut = len(others) - (N0 - 1)
         lists = {R: [order[0]] + others[cut:]}
         for h, c in enumerate(comp):
             lists[c] = others[:cut][h::len(comp)]
@@ -153,28 +160,19 @@ def _plan(T, topo):
     return P
 
 
-def _relay(g, core, T, topo, P, r, j):
-    dsts = [P["owner"][d][r] for d in P["cross"][r][j]]
-    if not dsts:
-        return
-    m = _pick(topo.mask(core, dsts[0]), 8)
-    g.wait_ge(T.sem.wrs, 8)
-    g.remote_dma_fused([RemoteDMATransfer(dst_ids=_ids(topo, dsts, core), dma_engine_mask=m, remote_sem=T.sem["w%d" % r],
-                                          srcs=[T.wr[:, :]], dsts=[T.wt[:, r * 256:r * 256 + 256]] * len(dsts))],
-                       local_sem=T.sem.loc)
-    g.wait_ge(T.sem.loc, 8)
+def _weng(P, c):
+    return PENG if P["role"][c][0] == "comp" else WENG
 
 
-def _words(g, core, T, topo, P, r, i):
+def _words_vec(g, core, T, P, r, own):
     sem, V, PE = T.sem, g.vector, g.tensor
-    nw = len(P["wh"][r])
-    c0, c1 = i * 128 // nw, (i + 1) * 128 // nw
+    c0, c1 = P["cols"][core]
     nc = c1 - c0
     route = T.tables["ROUTE"][r]
     cnt = [0]
 
     def fill(ap, v):
-        V.memset(ap, v).then_inc(sem.cs, 1)
+        V.memset(ap, v).then_inc(sem.wc, 1)
         cnt[0] += 1
     fill(T.lr[:, :], 0.0)
     fill(T.lb[0:1, 0:56], 1.0)
@@ -183,20 +181,20 @@ def _words(g, core, T, topo, P, r, i):
     fill(T.mag[:, 0:nc], MAGIC)
     fill(T.tin[:, 0:nc], TINY)
     fill(T.zf[:, 0:nc], 0.0)
-    V.wait_ge(sem.cs, cnt[0])
+    V.wait_ge(sem.wc, cnt[0])
     for q in range(6):
         fill(T.lr[0:1, 24 + q:152:32], 2.0 ** (-(q + 2)))
-    V.wait_ge(sem.cs, cnt[0])
-    V.tensor_tensor(T.lp[:, :], T.lr[:, :], T.lb[:, :], AluOpType.mult).then_inc(sem.cs, 1)
+    V.wait_ge(sem.wc, cnt[0])
+    V.tensor_tensor(T.lp[:, :], T.lr[:, :], T.lb[:, :], AluOpType.mult).then_inc(sem.wc, 1)
     cnt[0] += 1
     for k in range(5):
         for c in range(nc):
             fill(T.rw[0:1, k * nc + c:k * nc + c + 1], _word(route, k, c0 + c))
-    PE.wait_ge(sem.cs, cnt[0])
-    u = T.ph0[:, 0:nc]
+    PE.wait_ge(sem.wc, cnt[0])
+    u = T.pg0[:, 0:nc]
     for k in range(5):
         PE.matmul(u, T.lp[0:1, 24 - 6 * k:152 - 6 * k], T.rw[0:1, k * nc:(k + 1) * nc], k == 0, k == 4).then_inc(sem.hp, 1)
-    V.wait_ge(sem.cs, cnt[0])
+    V.wait_ge(sem.wc, cnt[0])
     V.wait_ge(sem.hp, 5)
     steps = [(T.a1, u, T.mag, AluOpType.add), (T.a2, T.a1, T.mag, AluOpType.subtract), (T.a3, T.a2, u, AluOpType.subtract),
              (T.a4, T.a3, T.tin, AluOpType.min), (T.fo, T.a4, T.zf, AluOpType.max)]
@@ -206,12 +204,33 @@ def _words(g, core, T, topo, P, r, i):
         V.tensor_tensor(o[:, 0:nc], a, b, op).then_inc(sem.hv, 1)
         if s < 4:
             V.wait_ge(sem.hv, s + 1)
-    dsts = [P["cores"][r]] + P["comp"][r]
-    m = _pick(topo.mask(core, dsts[0]), WENG)
-    g.wait_ge(sem.hv, 5)
-    g.remote_dma_fused([RemoteDMATransfer(dst_ids=_ids(topo, dsts, core), dma_engine_mask=m, remote_sem=sem.fa,
-                                          srcs=[T.fo[:, 0:nc]], dsts=[T.fb[:, c0:c1]] * len(dsts))], local_sem=sem.loc)
-    g.wait_ge(sem.loc, WENG)
+    if own:
+        V.tensor_tensor(T.fb[:, c0:c1], T.a4[:, 0:nc], T.zf[:, 0:nc], AluOpType.max).then_inc(sem.hv, 1)
+        return 6
+    return 5
+
+
+def _words_send(g, core, T, topo, P, r, hv):
+    sem = T.sem
+    c0, c1 = P["cols"][core]
+    dsts = [c for c in [P["cores"][r]] + P["comp"][r] if c != core]
+    eng = _weng(P, core)
+    g.wait_ge(sem.hv, hv)
+    g.remote_dma_fused([RemoteDMATransfer(dst_ids=_ids(topo, dsts, core), dma_engine_mask=_pick(topo.mask(core, dsts[0]), eng),
+                                          remote_sem=sem.fa, srcs=[T.fo[:, 0:c1 - c0]], dsts=[T.fb[:, c0:c1]] * len(dsts))],
+                       local_sem=sem.loc)
+    return eng
+
+
+def _relay(g, core, T, topo, P, r, j):
+    loc = _words_send(g, core, T, topo, P, r, _words_vec(g, core, T, P, r, False))
+    dsts = [P["owner"][d][r] for d in P["cross"][r][j]]
+    m = _pick(topo.mask(core, dsts[0]), 8)
+    g.wait_ge(T.sem.wrs, 8)
+    g.remote_dma_fused([RemoteDMATransfer(dst_ids=_ids(topo, dsts, core), dma_engine_mask=m, remote_sem=T.sem["w%d" % r],
+                                          srcs=[T.wr[:, :]], dsts=[T.wt[:, r * 256:r * 256 + 256]] * len(dsts))],
+                       local_sem=T.sem.loc)
+    g.wait_ge(T.sem.loc, loc + 8)
 
 
 def _compute(g, core, T, topo, P, r, h):
@@ -225,18 +244,17 @@ def _compute(g, core, T, topo, P, r, h):
     nh = len(comp)
     ph, pg = [T.ph0, T.ph1, T.ph2], [T.pg0, T.pg1, T.pg2]
     o = r * 256
-    nx = 32 if nh else 16
     if is_rank:
         S.dma_start(T.wt[:, o:o + 128], T.w1[:, :]).then_inc(sem.ldw, 16)
         A.dma_start(T.wt[:, o + 128:o + 256], T.w2[:, :]).then_inc(sem.ldw, 16)
         S.dma_start(T.xg[:, 0:512], T.x[:, :]).then_inc(sem.ldx, 16)
         A.dma_start(T.grow[:, :], T.gate[:, :]).then_inc(sem.ldg, 16)
-        if nh:
-            A.dma_start(T.xg[:, 512:524], T.gate[:, :]).then_inc(sem.ldx, 16)
+        A.dma_start(T.xg[:, 512:524], T.gate[:, :]).then_inc(sem.ldx, 16)
     else:
         S.wait_ge(sem.xa, 8)
         S.dma_start(T.grow[:, :], T.xg[:, 512:524]).then_inc(sem.ldg, 16)
     loc = 0
+    hv = 0
     if is_rank:
         src = T.wt[:, o:o + 256]
         sd = [P["owner"][d][r] for d in P["same"][r]]
@@ -249,12 +267,13 @@ def _compute(g, core, T, topo, P, r, h):
                               srcs=[src], dsts=[T.wr[:, :]] * len(rel)),
             RemoteDMATransfer(dst_ids=_ids(topo, sd, R), dma_engine_mask=off, remote_sem=sem["w%d" % r],
                               srcs=[src], dsts=[src] * len(sd))], local_sem=sem.loc)
-        loc += 16
-        if nh:
-            g.wait_ge(sem.ldx, nx)
-            g.remote_dma_fused([RemoteDMATransfer(dst_ids=_ids(topo, comp, R), dma_engine_mask=on, remote_sem=sem.xa,
-                                                  srcs=[T.xg[:, :]], dsts=[T.xg[:, :]] * nh)], local_sem=sem.loc)
-            loc += 8
+        g.wait_ge(sem.ldx, 32)
+        g.remote_dma_fused([RemoteDMATransfer(dst_ids=_ids(topo, comp, R), dma_engine_mask=on, remote_sem=sem.xa,
+                                              srcs=[T.xg[:, :]], dsts=[T.xg[:, :]] * nh)], local_sem=sem.loc)
+        loc += 24
+    else:
+        hv = _words_vec(g, core, T, P, r, True)
+        loc += _words_send(g, core, T, topo, P, r, hv)
     cnt = [0]
 
     def fill(ap, v):
@@ -264,17 +283,17 @@ def _compute(g, core, T, topo, P, r, h):
     fill(T.ip[:, :], 0.0)
     fill(T.one[:, :], BIG)
     fill(T.zer[:, :], 0.0)
-    if is_rank and nh:
+    if is_rank:
         fill(T.ids[:, :], 0.0)
     V.wait_ge(sem.cs, cnt[0])
     for b in range(4):
         fill(T.ap[0:1, 27 + 32 * b:30 + 32 * b], 1.0)
     fill(T.ip[0:1, 98:126:3], 1.0)
-    if is_rank and nh:
+    if is_rank:
         fill(T.ids[:, 0:1], 1.0)
     ncs = cnt[0]
     V.wait_ge(sem.cs, ncs)
-    if is_rank and nh:
+    if is_rank:
         S.wait_ge(sem.cs, ncs)
         S.dma_start(T.idd[:, :], T.ids[:, :]).then_inc(sem.i1, 16)
         S.wait_ge(sem.i1, 16)
@@ -331,7 +350,7 @@ def _compute(g, core, T, topo, P, r, h):
                         AluOpType.mult).then_inc(sem["mu_%d" % k], 1)
 
     if is_rank:
-        PE.wait_ge(sem.ldx, nx)
+        PE.wait_ge(sem.ldx, 32)
     else:
         PE.wait_ge(sem.xa, 8)
     PE.wait_ge(sem.sv, nb)
@@ -345,7 +364,7 @@ def _compute(g, core, T, topo, P, r, h):
         if k >= 1:
             mm2(k - 1)
     mm2(n - 1)
-    if is_rank and nh:
+    if is_rank:
         PE.wait_ge(sem.i2, 16)
         for j in range(nh):
             PE.wait_ge(sem["pa%d" % j], PENG)
@@ -353,7 +372,9 @@ def _compute(g, core, T, topo, P, r, h):
 
     for k in range(n1):
         relu(k)
-    V.wait_ge(sem.fa, WENG * len(P["wh"][r]))
+    V.wait_ge(sem.fa, sum(_weng(P, c) for c in P["wh"][r] if c != core))
+    if hv:
+        V.wait_ge(sem.hv, hv)
     V.wait_ge(sem.gl, 12)
     for b in range(4):
         V.tensor_tensor(T.gm[:, 128 * b:128 * b + 128], T.fb[:, :], T.pgl[:, 128 * b:128 * b + 128],
@@ -363,14 +384,18 @@ def _compute(g, core, T, topo, P, r, h):
             relu(k)
         mult(k)
     V.wait_ge(sem.m2, tot)
-    V.tensor_copy(T.yo[:, :], T.py[:, :]).then_inc(sem.ev, 1)
+    V.tensor_copy(T.yo[:, 0:256], T.py[:, 0:256]).then_inc(sem.ev0, 1)
+    V.tensor_copy(T.yo[:, 256:512], T.py[:, 256:512]).then_inc(sem.ev1, 1)
     if is_rank:
-        S.wait_ge(sem.ev, 1)
-        S.dma_start(T.y[:, :], T.yo[:, :]).then_inc(sem.st, 16)
-        S.wait_ge(sem.st, 16)
+        S.wait_ge(sem.ev0, 1)
+        S.dma_start(T.y[:, 0:256], T.yo[:, 0:256]).then_inc(sem.st, 16)
+        A.wait_ge(sem.ev1, 1)
+        A.dma_start(T.y[:, 256:512], T.yo[:, 256:512]).then_inc(sem.st, 16)
+        S.wait_ge(sem.st, 32)
     else:
         rid, pid = topo.addr(R, core)
-        g.wait_ge(sem.ev, 1)
+        g.wait_ge(sem.ev0, 1)
+        g.wait_ge(sem.ev1, 1)
         g.remote_dma(T.part[:, h * 512:h * 512 + 512], T.yo[:, :], sem["pa%d" % h], sem.loc, pid, rid,
                      _pick(topo.mask(core, R), PENG))
         loc += PENG
@@ -385,6 +410,6 @@ def rank_program(g, core, T, topo):
     if kind == "relay":
         _relay(g, core, T, topo, P, r, i)
     elif kind == "word":
-        _words(g, core, T, topo, P, r, i)
+        g.wait_ge(T.sem.loc, _words_send(g, core, T, topo, P, r, _words_vec(g, core, T, P, r, False)))
     else:
         _compute(g, core, T, topo, P, r, i)

@@ -1,55 +1,55 @@
 from concourse.bass import DstId, RemoteDMATransfer
-from concourse.mybir import AluOpType
+from concourse.mybir import AluOpType, ActivationFunctionType
 
 NSIM = 256
 NH = 2
 N0 = 6
 NREL = 2
+NDIR = 3
 NIDLE = 13
 WENG = 8
 PENG = 16
 NCMAX = 8
+NG = 4
+HW = 256
 BIG, TINY, MAGIC = 2.0 ** 25, 2.0 ** -25, 1.5 * 2.0 ** 23
 
 SCRATCH = {
-    "xg": ("sbuf", [128, 524], "bfloat16"),
+    "xg": ("sbuf", [128, 640], "bfloat16"),
     "wt": ("sbuf", [128, 2560], "bfloat16"),
     "wr": ("sbuf", [128, 256], "bfloat16"),
-    "rl": ("sbuf", [128, 5120], "bfloat16"),
-    "sg": ("sbuf", [128, 5120], "bfloat16"),
-    "zer": ("sbuf", [128, 512], "bfloat16"),
+    "rl": ("sbuf", [128, 512 * N0], "bfloat16"),
+    "sg": ("sbuf", [128, 512 * N0], "bfloat16"),
     "fb": ("sbuf", [128, 128], "bfloat16"),
+    "gd": ("sbuf", [128, 128], "bfloat16"),
     "gm": ("sbuf", [128, 512], "bfloat16"),
     "sel": ("sbuf", [128, 1280], "bfloat16"),
     "grow": ("sbuf", [1, 1536], "bfloat16"),
     "ap": ("sbuf", [1, 155], "bfloat16"),
     "ip": ("sbuf", [1, 226], "bfloat16"),
     "one": ("sbuf", [1, 128], "bfloat16"),
-    "lr": ("sbuf", [1, 152], "float32"),
-    "lb": ("sbuf", [1, 152], "float32"),
     "lp": ("sbuf", [1, 152], "float32"),
+    "pat": ("sbuf", [1, 2], "float32"),
     "rw": ("sbuf", [1, 5 * NCMAX], "float32"),
-    "mag": ("sbuf", [128, NCMAX], "float32"),
-    "tin": ("sbuf", [128, NCMAX], "float32"),
-    "zf": ("sbuf", [128, NCMAX], "float32"),
     "a1": ("sbuf", [128, NCMAX], "float32"),
     "a2": ("sbuf", [128, NCMAX], "float32"),
     "a3": ("sbuf", [128, NCMAX], "float32"),
-    "a4": ("sbuf", [128, NCMAX], "float32"),
     "fo": ("sbuf", [128, NCMAX], "bfloat16"),
     "part": ("sbuf", [128, 512 * max(NH, 1)], "bfloat16"),
     "ids": ("sbuf", [128, 129], "bfloat16"),
     "idd": ("dram", [129, 128], "bfloat16"),
     "ident": ("sbuf", [128, 128], "bfloat16"),
     "yo": ("sbuf", [128, 512], "bfloat16"),
-    "ph0": ("psum", [128, 512], "float32"), "ph1": ("psum", [128, 512], "float32"), "ph2": ("psum", [128, 512], "float32"),
-    "pg0": ("psum", [128, 512], "float32"), "pg1": ("psum", [128, 512], "float32"), "pg2": ("psum", [128, 512], "float32"),
-    "py": ("psum", [128, 512], "float32"), "pgl": ("psum", [128, 512], "float32"),
+    "ph0": ("psum", [128, 512], "float32"), "ph1": ("psum", [128, 512], "float32"),
+    "pg0": ("psum", [128, 512], "float32"), "pg1": ("psum", [128, 512], "float32"),
+    "pg2": ("psum", [128, 512], "float32"), "pg3": ("psum", [128, 512], "float32"),
+    "py0": ("psum", [128, 512], "float32"), "py1": ("psum", [128, 512], "float32"),
 }
-SEMAPHORES = (["cs", "wc", "se", "sv", "gl", "ldx", "ldw", "ldg", "xa", "wrs", "fa", "gms", "m2", "ev0", "ev1", "st", "loc",
-               "hp", "hv", "i1", "i2"]
+SEMAPHORES = (["cs", "ci", "gs", "gp", "wc", "wa", "wp", "se", "sv", "gl", "ldx", "ldw", "ldg", "xa", "wrs", "fa", "gms", "m20",
+               "m21", "ev0", "ev1", "st", "loc", "hp", "hv", "i1", "i2"]
               + ["w%d" % e for e in range(10)] + ["pa%d" % h for h in range(max(NH, 1))]
-              + ["%s_%d" % (s, k) for s in ("m1", "rl", "gb", "mu") for k in range(10)])
+              + ["gb_%d" % k for k in range(N0)]
+              + ["%s_%d_%d" % (s, k, f) for s in ("m1", "rl", "mu") for k in range(N0) for f in range(2)])
 
 _CACHE = {}
 
@@ -104,7 +104,8 @@ def _plan(T, topo):
         cross = [d for d in range(n) if d != r and not topo.may_write(R, cores[d])]
         ports = [c for c in mine if all(topo.may_write(c, cores[d]) for d in cross)]
         far = [c for c in ports if topo.die(c) != topo.die(R)]
-        relays = (far or ports)[:NREL]
+        near = [c for c in ports if topo.die(c) == topo.die(R)]
+        relays = ([far[0], near[-1]] if far and near else ports)[:NREL]
         comp = [c for c in mine if c not in relays and topo.die(c) == topo.die(R)][:NH]
         rest = [c for c in mine if c not in relays and c not in comp]
         onchip = len(rest)
@@ -124,9 +125,12 @@ def _plan(T, topo):
         same.sort(key=lambda d: (d - r) % n)
         cross.sort(key=lambda d: (d - r) % n)
         arr[r][r] = (0, 0)
+        same, extra = same[:NDIR], same[NDIR:]
         for p_, d in enumerate(same):
             arr[d][r] = (1, p_)
         split = [cross[j::len(relays)] for j in range(len(relays))]
+        for d in extra:
+            min(split, key=len).append(d)
         for part in split:
             for p_, d in enumerate(part):
                 arr[d][r] = (2, p_)
@@ -165,49 +169,53 @@ def _weng(P, c):
 
 
 def _words_vec(g, core, T, P, r, own):
-    sem, V, PE = T.sem, g.vector, g.tensor
+    sem, V, PE, A = T.sem, g.vector, g.tensor, g.scalar
     c0, c1 = P["cols"][core]
     nc = c1 - c0
     route = T.tables["ROUTE"][r]
-    cnt = [0]
-
-    def fill(ap, v):
-        V.memset(ap, v).then_inc(sem.wc, 1)
-        cnt[0] += 1
-    fill(T.lr[:, :], 0.0)
-    fill(T.lb[0:1, 0:56], 1.0)
-    for b in range(1, 4):
-        fill(T.lb[0:1, 24 + 32 * b:56 + 32 * b], 2.0 ** (-6 * b))
-    fill(T.mag[:, 0:nc], MAGIC)
-    fill(T.tin[:, 0:nc], TINY)
-    fill(T.zf[:, 0:nc], 0.0)
-    V.wait_ge(sem.wc, cnt[0])
+    wd = [_word(route, k, c0 + c) for k in range(5) for c in range(nc)]
+    pairs = [(j, min(j + 2, len(wd))) for j in range(0, len(wd), 2)]
+    nv = max(0, (len(pairs) - 10) // 2)
+    pa, pv = pairs[:len(pairs) - nv], pairs[len(pairs) - nv:]
+    V.memset(T.pat[0:1, 0:1], 0.0).then_inc(sem.wp, 1)
+    V.memset(T.pat[0:1, 1:2], 1.0).then_inc(sem.wp, 1)
+    A.wait_ge(sem.wp, 2)
+    for j0, j1 in pa:
+        A.activation(T.rw[0:1, j0:j1], T.pat[0:1, 0:j1 - j0], ActivationFunctionType.Identity,
+                     bias=float(wd[j0]), scale=float(wd[j1 - 1] - wd[j0])).then_inc(sem.wa, 1)
+    cnt = 1
+    V.memset(T.lp[:, :], 0.0).then_inc(sem.wc, 1)
+    V.wait_ge(sem.wc, cnt)
     for q in range(6):
-        fill(T.lr[0:1, 24 + q:152:32], 2.0 ** (-(q + 2)))
-    V.wait_ge(sem.wc, cnt[0])
-    V.tensor_tensor(T.lp[:, :], T.lr[:, :], T.lb[:, :], AluOpType.mult).then_inc(sem.wc, 1)
-    cnt[0] += 1
-    for k in range(5):
-        for c in range(nc):
-            fill(T.rw[0:1, k * nc + c:k * nc + c + 1], _word(route, k, c0 + c))
-    PE.wait_ge(sem.wc, cnt[0])
-    u = T.pg0[:, 0:nc]
+        V.memset(T.lp[0:1, 24 + q:152:32], 2.0 ** (-(q + 2))).then_inc(sem.wc, 1)
+        cnt += 1
+    V.wait_ge(sem.wc, cnt)
+    for b in range(1, 4):
+        V.tensor_scalar(T.lp[0:1, 24 + 32 * b:56 + 32 * b], T.lp[0:1, 24 + 32 * b:56 + 32 * b], 2.0 ** (-6 * b), None,
+                        AluOpType.mult).then_inc(sem.wc, 1)
+        cnt += 1
+    V.wait_ge(sem.wp, 2)
+    for j0, j1 in pv:
+        V.tensor_scalar(T.rw[0:1, j0:j1], T.pat[0:1, 0:j1 - j0], float(wd[j1 - 1] - wd[j0]), float(wd[j0]),
+                        AluOpType.mult, AluOpType.add).then_inc(sem.wc, 1)
+        cnt += 1
+    PE.wait_ge(sem.wc, cnt)
+    PE.wait_ge(sem.wa, len(pa))
+    u = T.py0[:, 0:nc]
     for k in range(5):
         PE.matmul(u, T.lp[0:1, 24 - 6 * k:152 - 6 * k], T.rw[0:1, k * nc:(k + 1) * nc], k == 0, k == 4).then_inc(sem.hp, 1)
-    V.wait_ge(sem.wc, cnt[0])
     V.wait_ge(sem.hp, 5)
-    steps = [(T.a1, u, T.mag, AluOpType.add), (T.a2, T.a1, T.mag, AluOpType.subtract), (T.a3, T.a2, u, AluOpType.subtract),
-             (T.a4, T.a3, T.tin, AluOpType.min), (T.fo, T.a4, T.zf, AluOpType.max)]
-    for s, (o, a, b, op) in enumerate(steps):
-        a = a if a is u else a[:, 0:nc]
-        b = b if b is u else b[:, 0:nc]
-        V.tensor_tensor(o[:, 0:nc], a, b, op).then_inc(sem.hv, 1)
-        if s < 4:
-            V.wait_ge(sem.hv, s + 1)
+    V.tensor_scalar(T.a1[:, 0:nc], u, MAGIC, None, AluOpType.add).then_inc(sem.hv, 1)
+    V.wait_ge(sem.hv, 1)
+    V.tensor_scalar(T.a2[:, 0:nc], T.a1[:, 0:nc], MAGIC, None, AluOpType.subtract).then_inc(sem.hv, 1)
+    V.wait_ge(sem.hv, 2)
+    V.tensor_tensor(T.a3[:, 0:nc], T.a2[:, 0:nc], u, AluOpType.subtract).then_inc(sem.hv, 1)
+    V.wait_ge(sem.hv, 3)
+    V.tensor_scalar(T.fo[:, 0:nc], T.a3[:, 0:nc], TINY, 0.0, AluOpType.min, AluOpType.max).then_inc(sem.hv, 1)
     if own:
-        V.tensor_tensor(T.fb[:, c0:c1], T.a4[:, 0:nc], T.zf[:, 0:nc], AluOpType.max).then_inc(sem.hv, 1)
-        return 6
-    return 5
+        V.tensor_scalar(T.fb[:, c0:c1], T.a3[:, 0:nc], TINY, 0.0, AluOpType.min, AluOpType.max).then_inc(sem.hv, 1)
+        return 5
+    return 4
 
 
 def _words_send(g, core, T, topo, P, r, hv):
@@ -225,7 +233,10 @@ def _words_send(g, core, T, topo, P, r, hv):
 def _relay(g, core, T, topo, P, r, j):
     loc = _words_send(g, core, T, topo, P, r, _words_vec(g, core, T, P, r, False))
     dsts = [P["owner"][d][r] for d in P["cross"][r][j]]
-    m = _pick(topo.mask(core, dsts[0]), 8)
+    m = topo.mask(core, dsts[0])
+    for d in dsts:
+        m &= topo.mask(core, d)
+    m = _pick(m, 8)
     g.wait_ge(T.sem.wrs, 8)
     g.remote_dma_fused([RemoteDMATransfer(dst_ids=_ids(topo, dsts, core), dma_engine_mask=m, remote_sem=T.sem["w%d" % r],
                                           srcs=[T.wr[:, :]], dsts=[T.wt[:, r * 256:r * 256 + 256]] * len(dsts))],
@@ -242,17 +253,14 @@ def _compute(g, core, T, topo, P, r, h):
     n1 = len([1 for e, hp in L if hp <= 1])
     comp = P["comp"][r]
     nh = len(comp)
-    ph, pg = [T.ph0, T.ph1, T.ph2], [T.pg0, T.pg1, T.pg2]
+    ph, pg, py = [T.ph0, T.ph1], [T.pg0, T.pg1, T.pg2, T.pg3], [T.py0, T.py1]
+    pgl = T.pg3[:, 0:128]
     o = r * 256
     if is_rank:
         S.dma_start(T.wt[:, o:o + 128], T.w1[:, :]).then_inc(sem.ldw, 16)
+        A.dma_start(T.grow[:, :], T.gate[:, :]).then_inc(sem.ldg, 16)
         A.dma_start(T.wt[:, o + 128:o + 256], T.w2[:, :]).then_inc(sem.ldw, 16)
         S.dma_start(T.xg[:, 0:512], T.x[:, :]).then_inc(sem.ldx, 16)
-        A.dma_start(T.grow[:, :], T.gate[:, :]).then_inc(sem.ldg, 16)
-        A.dma_start(T.xg[:, 512:524], T.gate[:, :]).then_inc(sem.ldx, 16)
-    else:
-        S.wait_ge(sem.xa, 8)
-        S.dma_start(T.grow[:, :], T.xg[:, 512:524]).then_inc(sem.ldg, 16)
     loc = 0
     hv = 0
     if is_rank:
@@ -262,62 +270,68 @@ def _compute(g, core, T, topo, P, r, h):
         off = _pick(topo.mask(R, sd[0]), 8)
         on = _pick(topo.mask(R, rel[0]) & ~off, 8)
         g.wait_ge(sem.ldw, 32)
-        g.remote_dma_fused([
-            RemoteDMATransfer(dst_ids=_ids(topo, rel, R), dma_engine_mask=on, remote_sem=sem.wrs,
-                              srcs=[src], dsts=[T.wr[:, :]] * len(rel)),
-            RemoteDMATransfer(dst_ids=_ids(topo, sd, R), dma_engine_mask=off, remote_sem=sem["w%d" % r],
-                              srcs=[src], dsts=[src] * len(sd))], local_sem=sem.loc)
-        g.wait_ge(sem.ldx, 32)
-        g.remote_dma_fused([RemoteDMATransfer(dst_ids=_ids(topo, comp, R), dma_engine_mask=on, remote_sem=sem.xa,
-                                              srcs=[T.xg[:, :]], dsts=[T.xg[:, :]] * nh)], local_sem=sem.loc)
-        loc += 24
+        g.remote_dma_fused([RemoteDMATransfer(dst_ids=_ids(topo, rel, R), dma_engine_mask=on, remote_sem=sem.wrs,
+                                              srcs=[src], dsts=[T.wr[:, :]] * len(rel))], local_sem=sem.loc)
+        g.wait_ge(sem.ldx, 16)
+        g.wait_ge(sem.gs, 1)
+        g.remote_dma_fused([RemoteDMATransfer(dst_ids=_ids(topo, [c], R), dma_engine_mask=m_, remote_sem=sem.xa,
+                                              srcs=[T.xg[:, :]], dsts=[T.xg[:, :]]) for c, m_ in zip(comp, (on, off))],
+                           local_sem=sem.loc)
+        g.remote_dma_fused([RemoteDMATransfer(dst_ids=_ids(topo, sd, R), dma_engine_mask=off, remote_sem=sem["w%d" % r],
+                                              srcs=[src], dsts=[src] * len(sd))], local_sem=sem.loc)
+        loc += 32
     else:
         hv = _words_vec(g, core, T, P, r, True)
         loc += _words_send(g, core, T, topo, P, r, hv)
+    if is_rank:
+        V.memset(T.ip[:, :], 0.0).then_inc(sem.ci, 1)
+        V.wait_ge(sem.ci, 1)
+        V.memset(T.ip[0:1, 98:126:3], 1.0).then_inc(sem.ci, 1)
+        PE.wait_ge(sem.ci, 2)
+        PE.wait_ge(sem.ldg, 16)
+        for b in range(4):
+            for i in range(3):
+                PE.matmul(pgl, T.ip[0:1, 98 - 32 * b - i:226 - 32 * b - i],
+                          T.grow[0:1, 512 * i + 128 * b:512 * i + 128 * b + 128], b + i == 0, b + i == 5).then_inc(sem.gl, 1)
     cnt = [0]
 
     def fill(ap, v):
         V.memset(ap, v).then_inc(sem.cs, 1)
         cnt[0] += 1
     fill(T.ap[:, :], 0.0)
-    fill(T.ip[:, :], 0.0)
     fill(T.one[:, :], BIG)
-    fill(T.zer[:, :], 0.0)
     if is_rank:
         fill(T.ids[:, :], 0.0)
     V.wait_ge(sem.cs, cnt[0])
     for b in range(4):
         fill(T.ap[0:1, 27 + 32 * b:30 + 32 * b], 1.0)
-    fill(T.ip[0:1, 98:126:3], 1.0)
     if is_rank:
         fill(T.ids[:, 0:1], 1.0)
+    fill(T.gm[:, :], 0.0)
     ncs = cnt[0]
     V.wait_ge(sem.cs, ncs)
     if is_rank:
+        V.wait_ge(sem.gl, 12)
+        V.tensor_copy(T.xg[:, 512:640], pgl).then_inc(sem.gs, 1)
         S.wait_ge(sem.cs, ncs)
         S.dma_start(T.idd[:, :], T.ids[:, :]).then_inc(sem.i1, 16)
         S.wait_ge(sem.i1, 16)
         S.dma_start(T.ident[:, :], T.idd[0:128, :]).then_inc(sem.i2, 16)
     PE.wait_ge(sem.cs, ncs)
     for k, (e, hp) in enumerate(L):
-        PE.matmul(ph[k // 4][:, (k % 4) * 128:(k % 4) * 128 + 128], T.ap[0:1, 27 - 3 * e:155 - 3 * e], T.one[0:1, :],
+        PE.matmul(pg[k // 4][:, (k % 4) * 128:(k % 4) * 128 + 128], T.ap[0:1, 27 - 3 * e:155 - 3 * e], T.one[0:1, :],
                   True, True).then_inc(sem.se, 1)
     V.wait_ge(sem.se, n)
     nb = (n + 3) // 4
     for b in range(nb):
         w = min(4, n - 4 * b) * 128
-        V.tensor_copy(T.sel[:, b * 512:b * 512 + w], ph[b][:, 0:w]).then_inc(sem.sv, 1)
-    PE.wait_ge(sem.ldg, 16)
-    for b in range(4):
-        for i in range(3):
-            PE.matmul(T.pgl[:, 128 * b:128 * b + 128], T.ip[0:1, 98 - 32 * b - i:226 - 32 * b - i],
-                      T.grow[0:1, 512 * i + 128 * b:512 * i + 128 * b + 128], i == 0, i == 2).then_inc(sem.gl, 1)
+        V.tensor_copy(T.sel[:, b * 512:b * 512 + w], pg[b][:, 0:w]).then_inc(sem.sv, 1)
     tot = n + (nh if is_rank else 0)
-    done = [0]
+    done = [0, 0]
 
-    def acc(lhsT, rhs):
-        PE.matmul(T.py[:, :], lhsT, rhs, done[0] == 0, done[0] == tot - 1).then_inc(sem.m2, 1)
-        done[0] += 1
+    def acc(f, lhsT, rhs):
+        PE.matmul(py[f][:, 0:HW], lhsT, rhs, done[f] == 0, done[f] == tot - 1).then_inc(sem["m2%d" % f], 1)
+        done[f] += 1
 
     def mm1(k):
         e, hp = L[k]
@@ -325,72 +339,80 @@ def _compute(g, core, T, topo, P, r, h):
             PE.wait_ge(sem.ldw, 32)
         else:
             PE.wait_ge(sem["w%d" % e], 8)
-        if k >= 3:
-            PE.wait_ge(sem["rl_%d" % (k - 3)], 1)
-        PE.matmul(ph[k % 3][:, :], T.wt[:, e * 256:e * 256 + 128], T.xg[:, 0:512], True, True).then_inc(sem["m1_%d" % k], 1)
+        for f in range(2):
+            if k >= 1:
+                PE.wait_ge(sem["rl_%d_%d" % (k - 1, f)], 1)
+            PE.matmul(ph[f][:, 0:HW], T.wt[:, e * 256:e * 256 + 128], T.xg[:, f * HW:f * HW + HW],
+                      True, True).then_inc(sem["m1_%d_%d" % (k, f)], 1)
 
     def gb(k):
-        if k >= 3:
-            PE.wait_ge(sem["mu_%d" % (k - 3)], 1)
-        PE.matmul(pg[k % 3][:, :], T.sel[:, k * 128:k * 128 + 128], T.gm[:, :], True, True).then_inc(sem["gb_%d" % k], 1)
+        PE.matmul(pg[k % NG][:, :], T.sel[:, k * 128:k * 128 + 128], T.gm[:, :], True, True).then_inc(sem["gb_%d" % k], 1)
 
     def mm2(k):
         e = L[k][0]
-        PE.wait_ge(sem["mu_%d" % k], 1)
-        acc(T.wt[:, e * 256 + 128:e * 256 + 256], T.sg[:, k * 512:k * 512 + 512])
-
-    def relu(k):
-        V.wait_ge(sem["m1_%d" % k], 1)
-        V.tensor_tensor(T.rl[:, k * 512:k * 512 + 512], ph[k % 3][:, :], T.zer[:, :], AluOpType.max).then_inc(sem["rl_%d" % k], 1)
-
-    def mult(k):
-        V.wait_ge(sem["gb_%d" % k], 1)
-        V.wait_ge(sem["rl_%d" % k], 1)
-        V.tensor_tensor(T.sg[:, k * 512:k * 512 + 512], T.rl[:, k * 512:k * 512 + 512], pg[k % 3][:, :],
-                        AluOpType.mult).then_inc(sem["mu_%d" % k], 1)
+        for f in range(2):
+            PE.wait_ge(sem["mu_%d_%d" % (k, f)], 1)
+            acc(f, T.wt[:, e * 256 + 128:e * 256 + 256], T.sg[:, k * 512 + f * HW:k * 512 + f * HW + HW])
+        if k + NG < n:
+            gb(k + NG)
 
     if is_rank:
-        PE.wait_ge(sem.ldx, 32)
+        PE.wait_ge(sem.ldx, 16)
     else:
         PE.wait_ge(sem.xa, 8)
-    PE.wait_ge(sem.sv, nb)
     for k in range(n1):
         mm1(k)
     PE.wait_ge(sem.gms, 4)
-    for k in range(n):
-        if k >= n1:
-            mm1(k)
+    PE.wait_ge(sem.sv, nb)
+    for k in range(min(NG, n)):
         gb(k)
-        if k >= 1:
+    for k in range(n1):
+        mm2(k)
+    for k in range(n1, n):
+        mm1(k)
+        if k - 1 >= n1:
             mm2(k - 1)
-    mm2(n - 1)
     if is_rank:
         PE.wait_ge(sem.i2, 16)
         for j in range(nh):
             PE.wait_ge(sem["pa%d" % j], PENG)
-            acc(T.ident[:, :], T.part[:, j * 512:j * 512 + 512])
+            for f in range(2):
+                acc(f, T.ident[:, :], T.part[:, j * 512 + f * HW:j * 512 + f * HW + HW])
+    if n1 < n:
+        mm2(n - 1)
 
-    for k in range(n1):
-        relu(k)
+    for k in range(n):
+        for f in range(2):
+            A.wait_ge(sem["m1_%d_%d" % (k, f)], 1)
+            A.activation(T.rl[:, k * 512 + f * HW:k * 512 + f * HW + HW], ph[f][:, 0:HW],
+                         ActivationFunctionType.Relu).then_inc(sem["rl_%d_%d" % (k, f)], 1)
+
     V.wait_ge(sem.fa, sum(_weng(P, c) for c in P["wh"][r] if c != core))
     if hv:
         V.wait_ge(sem.hv, hv)
-    V.wait_ge(sem.gl, 12)
+    if is_rank:
+        V.wait_ge(sem.gs, 1)
+    else:
+        V.wait_ge(sem.xa, 8)
+    V.tensor_tensor(T.gd[:, :], T.fb[:, :], T.xg[:, 512:640], AluOpType.mult).then_inc(sem.gp, 1)
+    V.wait_ge(sem.gp, 1)
     for b in range(4):
-        V.tensor_tensor(T.gm[:, 128 * b:128 * b + 128], T.fb[:, :], T.pgl[:, 128 * b:128 * b + 128],
-                        AluOpType.mult).then_inc(sem.gms, 1)
+        V.tensor_copy(T.gm[32 * b:32 * b + 32, 128 * b:128 * b + 128], T.gd[32 * b:32 * b + 32, :]).then_inc(sem.gms, 1)
     for k in range(n):
-        if k >= n1:
-            relu(k)
-        mult(k)
-    V.wait_ge(sem.m2, tot)
-    V.tensor_copy(T.yo[:, 0:256], T.py[:, 0:256]).then_inc(sem.ev0, 1)
-    V.tensor_copy(T.yo[:, 256:512], T.py[:, 256:512]).then_inc(sem.ev1, 1)
+        V.wait_ge(sem["gb_%d" % k], 1)
+        for f in range(2):
+            V.wait_ge(sem["rl_%d_%d" % (k, f)], 1)
+            V.tensor_tensor(T.sg[:, k * 512 + f * HW:k * 512 + f * HW + HW], T.rl[:, k * 512 + f * HW:k * 512 + f * HW + HW],
+                            pg[k % NG][:, f * HW:f * HW + HW], AluOpType.mult).then_inc(sem["mu_%d_%d" % (k, f)], 1)
+    V.wait_ge(sem.m20, tot)
+    V.tensor_copy(T.yo[:, 0:HW], T.py0[:, 0:HW]).then_inc(sem.ev0, 1)
+    A.wait_ge(sem.m21, tot)
+    A.activation(T.yo[:, HW:2 * HW], T.py1[:, 0:HW], ActivationFunctionType.Copy).then_inc(sem.ev1, 1)
     if is_rank:
         S.wait_ge(sem.ev0, 1)
-        S.dma_start(T.y[:, 0:256], T.yo[:, 0:256]).then_inc(sem.st, 16)
+        S.dma_start(T.y[:, 0:HW], T.yo[:, 0:HW]).then_inc(sem.st, 16)
         A.wait_ge(sem.ev1, 1)
-        A.dma_start(T.y[:, 256:512], T.yo[:, 256:512]).then_inc(sem.st, 16)
+        A.dma_start(T.y[:, HW:2 * HW], T.yo[:, HW:2 * HW]).then_inc(sem.st, 16)
         S.wait_ge(sem.st, 32)
     else:
         rid, pid = topo.addr(R, core)

from concourse.bass import DstId, RemoteDMATransfer
from concourse.mybir import AluOpType, ActivationFunctionType

NSIM = 256
NH = 2
N0 = 6
NREL = 2
NDIR = 3
NIDLE = 13
WENG = 8
PENG = 16
NCMAX = 8
NG = 4
HW = 256
BIG, TINY, MAGIC = 2.0 ** 25, 2.0 ** -25, 1.5 * 2.0 ** 23

SCRATCH = {
    "xg": ("sbuf", [128, 640], "bfloat16"),
    "wt": ("sbuf", [128, 2560], "bfloat16"),
    "wr": ("sbuf", [128, 256], "bfloat16"),
    "rl": ("sbuf", [128, 512 * N0], "bfloat16"),
    "sg": ("sbuf", [128, 512 * N0], "bfloat16"),
    "fb": ("sbuf", [128, 128], "bfloat16"),
    "gd": ("sbuf", [128, 128], "bfloat16"),
    "gm": ("sbuf", [128, 512], "bfloat16"),
    "sel": ("sbuf", [128, 1280], "bfloat16"),
    "grow": ("sbuf", [1, 1536], "bfloat16"),
    "ap": ("sbuf", [1, 155], "bfloat16"),
    "ip": ("sbuf", [1, 226], "bfloat16"),
    "one": ("sbuf", [1, 128], "bfloat16"),
    "lp": ("sbuf", [1, 152], "float32"),
    "pat": ("sbuf", [1, 2], "float32"),
    "rw": ("sbuf", [1, 5 * NCMAX], "float32"),
    "a1": ("sbuf", [128, NCMAX], "float32"),
    "a2": ("sbuf", [128, NCMAX], "float32"),
    "a3": ("sbuf", [128, NCMAX], "float32"),
    "fo": ("sbuf", [128, NCMAX], "bfloat16"),
    "part": ("sbuf", [128, 512 * max(NH, 1)], "bfloat16"),
    "ids": ("sbuf", [128, 129], "bfloat16"),
    "idd": ("dram", [129, 128], "bfloat16"),
    "ident": ("sbuf", [128, 128], "bfloat16"),
    "yo": ("sbuf", [128, 512], "bfloat16"),
    "ph0": ("psum", [128, 512], "float32"), "ph1": ("psum", [128, 512], "float32"),
    "pg0": ("psum", [128, 512], "float32"), "pg1": ("psum", [128, 512], "float32"),
    "pg2": ("psum", [128, 512], "float32"), "pg3": ("psum", [128, 512], "float32"),
    "py0": ("psum", [128, 512], "float32"), "py1": ("psum", [128, 512], "float32"),
}
SEMAPHORES = (["cs", "ci", "gs", "gp", "wc", "wa", "wp", "se", "sv", "gl", "ldx", "ldw", "ldg", "xa", "wrs", "fa", "gms", "m20",
               "m21", "ev0", "ev1", "st", "loc", "hp", "hv", "i1", "i2"]
              + ["w%d" % e for e in range(10)] + ["pa%d" % h for h in range(max(NH, 1))]
              + ["gb_%d" % k for k in range(N0)]
              + ["%s_%d_%d" % (s, k, f) for s in ("m1", "rl", "mu") for k in range(N0) for f in range(2)])

_CACHE = {}


def _pick(mask, n):
    b = [i for i in range(32) if (mask >> i) & 1][:n]
    return sum(1 << i for i in b)


def _ids(topo, dsts, src):
    out = []
    for d in dsts:
        rid, pid = topo.addr(d, src)
        out.append(DstId(rid=rid, pnc=pid))
    return out


def _word(route, k, c):
    bits = 0
    for b in range(4):
        for x in range(2):
            for i in range(3):
                if route[128 * b + c][i] == 2 * k + x:
                    bits |= 1 << (6 * b + 3 * x + i)
    full = (1 << 23) - 1
    low = bits & full
    if bits >> 23:
        return -float(1 + 2 * (full ^ low))
    return float(1 + 2 * low)


def _plan(T, topo):
    if "p" in _CACHE:
        return _CACHE["p"]
    cores = list(T.cores)
    n = len(cores)

    def key(c):
        return (topo.host(c), topo.chip(c))
    bychip = {}
    for c in range(NSIM):
        bychip.setdefault(key(c), []).append(c)
    rankkeys = [key(c) for c in cores]
    idle = [c for k in sorted(bychip) if k not in rankkeys for c in bychip[k]]
    used = {}
    role = {}
    P = {"cores": cores, "role": role, "comp": [], "relays": [], "wh": [], "same": [], "cross": [], "lists": {}, "cols": {}}
    arr = [[None] * n for _ in range(n)]
    for r, R in enumerate(cores):
        mine = [c for c in bychip[key(R)] if c != R]
        same = [d for d in range(n) if d != r and topo.may_write(R, cores[d])]
        cross = [d for d in range(n) if d != r and not topo.may_write(R, cores[d])]
        ports = [c for c in mine if all(topo.may_write(c, cores[d]) for d in cross)]
        far = [c for c in ports if topo.die(c) != topo.die(R)]
        near = [c for c in ports if topo.die(c) == topo.die(R)]
        relays = ([far[0], near[-1]] if far and near else ports)[:NREL]
        comp = [c for c in mine if c not in relays and topo.die(c) == topo.die(R)][:NH]
        rest = [c for c in mine if c not in relays and c not in comp]
        onchip = len(rest)
        for c in idle:
            if len(rest) < onchip + NIDLE and c not in used and topo.same_plane(c, R) and topo.may_write(c, R):
                used[c] = 1
                rest.append(c)
        pos = 0
        for c in comp:
            P["cols"][c] = (pos, pos + 8)
            pos += 8
        for c in relays:
            P["cols"][c] = (pos, pos + 2)
            pos += 2
        for i, c in enumerate(rest):
            P["cols"][c] = (pos + i * (128 - pos) // len(rest), pos + (i + 1) * (128 - pos) // len(rest))
        same.sort(key=lambda d: (d - r) % n)
        cross.sort(key=lambda d: (d - r) % n)
        arr[r][r] = (0, 0)
        same, extra = same[:NDIR], same[NDIR:]
        for p_, d in enumerate(same):
            arr[d][r] = (1, p_)
        split = [cross[j::len(relays)] for j in range(len(relays))]
        for d in extra:
            min(split, key=len).append(d)
        for part in split:
            for p_, d in enumerate(part):
                arr[d][r] = (2, p_)
        for c in rest:
            role[c] = ("word", r, 0)
        role[R] = ("rank", r, 0)
        for h, c in enumerate(comp):
            role[c] = ("comp", r, h)
        for j, c in enumerate(relays):
            role[c] = ("relay", r, j)
        P["comp"].append(comp)
        P["relays"].append(relays)
        P["wh"].append(comp + relays + rest)
        P["same"].append(same)
        P["cross"].append(split)
    owner = [[None] * n for _ in range(n)]
    for d, R in enumerate(cores):
        order = sorted(range(n), key=lambda e: arr[d][e])
        others = order[1:]
        comp = P["comp"][d]
        cut = len(others) - (N0 - 1)
        lists = {R: [order[0]] + others[cut:]}
        for h, c in enumerate(comp):
            lists[c] = others[:cut][h::len(comp)]
        for c in lists:
            P["lists"][c] = [(e, arr[d][e][0]) for e in lists[c]]
            for e in lists[c]:
                owner[d][e] = c
    P["owner"] = owner
    _CACHE["p"] = P
    return P


def _weng(P, c):
    return PENG if P["role"][c][0] == "comp" else WENG


def _words_vec(g, core, T, P, r, own):
    sem, V, PE, A = T.sem, g.vector, g.tensor, g.scalar
    c0, c1 = P["cols"][core]
    nc = c1 - c0
    route = T.tables["ROUTE"][r]
    wd = [_word(route, k, c0 + c) for k in range(5) for c in range(nc)]
    pairs = [(j, min(j + 2, len(wd))) for j in range(0, len(wd), 2)]
    nv = max(0, (len(pairs) - 10) // 2)
    pa, pv = pairs[:len(pairs) - nv], pairs[len(pairs) - nv:]
    V.memset(T.pat[0:1, 0:1], 0.0).then_inc(sem.wp, 1)
    V.memset(T.pat[0:1, 1:2], 1.0).then_inc(sem.wp, 1)
    A.wait_ge(sem.wp, 2)
    for j0, j1 in pa:
        A.activation(T.rw[0:1, j0:j1], T.pat[0:1, 0:j1 - j0], ActivationFunctionType.Identity,
                     bias=float(wd[j0]), scale=float(wd[j1 - 1] - wd[j0])).then_inc(sem.wa, 1)
    cnt = 1
    V.memset(T.lp[:, :], 0.0).then_inc(sem.wc, 1)
    V.wait_ge(sem.wc, cnt)
    for q in range(6):
        V.memset(T.lp[0:1, 24 + q:152:32], 2.0 ** (-(q + 2))).then_inc(sem.wc, 1)
        cnt += 1
    V.wait_ge(sem.wc, cnt)
    for b in range(1, 4):
        V.tensor_scalar(T.lp[0:1, 24 + 32 * b:56 + 32 * b], T.lp[0:1, 24 + 32 * b:56 + 32 * b], 2.0 ** (-6 * b), None,
                        AluOpType.mult).then_inc(sem.wc, 1)
        cnt += 1
    V.wait_ge(sem.wp, 2)
    for j0, j1 in pv:
        V.tensor_scalar(T.rw[0:1, j0:j1], T.pat[0:1, 0:j1 - j0], float(wd[j1 - 1] - wd[j0]), float(wd[j0]),
                        AluOpType.mult, AluOpType.add).then_inc(sem.wc, 1)
        cnt += 1
    PE.wait_ge(sem.wc, cnt)
    PE.wait_ge(sem.wa, len(pa))
    u = T.py0[:, 0:nc]
    for k in range(5):
        PE.matmul(u, T.lp[0:1, 24 - 6 * k:152 - 6 * k], T.rw[0:1, k * nc:(k + 1) * nc], k == 0, k == 4).then_inc(sem.hp, 1)
    V.wait_ge(sem.hp, 5)
    V.tensor_scalar(T.a1[:, 0:nc], u, MAGIC, None, AluOpType.add).then_inc(sem.hv, 1)
    V.wait_ge(sem.hv, 1)
    V.tensor_scalar(T.a2[:, 0:nc], T.a1[:, 0:nc], MAGIC, None, AluOpType.subtract).then_inc(sem.hv, 1)
    V.wait_ge(sem.hv, 2)
    V.tensor_tensor(T.a3[:, 0:nc], T.a2[:, 0:nc], u, AluOpType.subtract).then_inc(sem.hv, 1)
    V.wait_ge(sem.hv, 3)
    V.tensor_scalar(T.fo[:, 0:nc], T.a3[:, 0:nc], TINY, 0.0, AluOpType.min, AluOpType.max).then_inc(sem.hv, 1)
    if own:
        V.tensor_scalar(T.fb[:, c0:c1], T.a3[:, 0:nc], TINY, 0.0, AluOpType.min, AluOpType.max).then_inc(sem.hv, 1)
        return 5
    return 4


def _words_send(g, core, T, topo, P, r, hv):
    sem = T.sem
    c0, c1 = P["cols"][core]
    dsts = [c for c in [P["cores"][r]] + P["comp"][r] if c != core]
    eng = _weng(P, core)
    g.wait_ge(sem.hv, hv)
    g.remote_dma_fused([RemoteDMATransfer(dst_ids=_ids(topo, dsts, core), dma_engine_mask=_pick(topo.mask(core, dsts[0]), eng),
                                          remote_sem=sem.fa, srcs=[T.fo[:, 0:c1 - c0]], dsts=[T.fb[:, c0:c1]] * len(dsts))],
                       local_sem=sem.loc)
    return eng


def _relay(g, core, T, topo, P, r, j):
    loc = _words_send(g, core, T, topo, P, r, _words_vec(g, core, T, P, r, False))
    dsts = [P["owner"][d][r] for d in P["cross"][r][j]]
    m = topo.mask(core, dsts[0])
    for d in dsts:
        m &= topo.mask(core, d)
    m = _pick(m, 8)
    g.wait_ge(T.sem.wrs, 8)
    g.remote_dma_fused([RemoteDMATransfer(dst_ids=_ids(topo, dsts, core), dma_engine_mask=m, remote_sem=T.sem["w%d" % r],
                                          srcs=[T.wr[:, :]], dsts=[T.wt[:, r * 256:r * 256 + 256]] * len(dsts))],
                       local_sem=T.sem.loc)
    g.wait_ge(T.sem.loc, loc + 8)


def _compute(g, core, T, topo, P, r, h):
    sem, V, PE, S, A = T.sem, g.vector, g.tensor, g.sync, g.scalar
    R = P["cores"][r]
    is_rank = core == R
    L = P["lists"][core]
    n = len(L)
    n1 = len([1 for e, hp in L if hp <= 1])
    comp = P["comp"][r]
    nh = len(comp)
    ph, pg, py = [T.ph0, T.ph1], [T.pg0, T.pg1, T.pg2, T.pg3], [T.py0, T.py1]
    pgl = T.pg3[:, 0:128]
    o = r * 256
    if is_rank:
        S.dma_start(T.wt[:, o:o + 128], T.w1[:, :]).then_inc(sem.ldw, 16)
        A.dma_start(T.grow[:, :], T.gate[:, :]).then_inc(sem.ldg, 16)
        A.dma_start(T.wt[:, o + 128:o + 256], T.w2[:, :]).then_inc(sem.ldw, 16)
        S.dma_start(T.xg[:, 0:512], T.x[:, :]).then_inc(sem.ldx, 16)
    loc = 0
    hv = 0
    if is_rank:
        src = T.wt[:, o:o + 256]
        sd = [P["owner"][d][r] for d in P["same"][r]]
        rel = P["relays"][r]
        off = _pick(topo.mask(R, sd[0]), 8)
        on = _pick(topo.mask(R, rel[0]) & ~off, 8)
        g.wait_ge(sem.ldw, 32)
        g.remote_dma_fused([RemoteDMATransfer(dst_ids=_ids(topo, rel, R), dma_engine_mask=on, remote_sem=sem.wrs,
                                              srcs=[src], dsts=[T.wr[:, :]] * len(rel))], local_sem=sem.loc)
        g.wait_ge(sem.ldx, 16)
        g.wait_ge(sem.gs, 1)
        g.remote_dma_fused([RemoteDMATransfer(dst_ids=_ids(topo, [c], R), dma_engine_mask=m_, remote_sem=sem.xa,
                                              srcs=[T.xg[:, :]], dsts=[T.xg[:, :]]) for c, m_ in zip(comp, (on, off))],
                           local_sem=sem.loc)
        g.remote_dma_fused([RemoteDMATransfer(dst_ids=_ids(topo, sd, R), dma_engine_mask=off, remote_sem=sem["w%d" % r],
                                              srcs=[src], dsts=[src] * len(sd))], local_sem=sem.loc)
        loc += 32
    else:
        hv = _words_vec(g, core, T, P, r, True)
        loc += _words_send(g, core, T, topo, P, r, hv)
    if is_rank:
        V.memset(T.ip[:, :], 0.0).then_inc(sem.ci, 1)
        V.wait_ge(sem.ci, 1)
        V.memset(T.ip[0:1, 98:126:3], 1.0).then_inc(sem.ci, 1)
        PE.wait_ge(sem.ci, 2)
        PE.wait_ge(sem.ldg, 16)
        for b in range(4):
            for i in range(3):
                PE.matmul(pgl, T.ip[0:1, 98 - 32 * b - i:226 - 32 * b - i],
                          T.grow[0:1, 512 * i + 128 * b:512 * i + 128 * b + 128], b + i == 0, b + i == 5).then_inc(sem.gl, 1)
    cnt = [0]

    def fill(ap, v):
        V.memset(ap, v).then_inc(sem.cs, 1)
        cnt[0] += 1
    fill(T.ap[:, :], 0.0)
    fill(T.one[:, :], BIG)
    if is_rank:
        fill(T.ids[:, :], 0.0)
    V.wait_ge(sem.cs, cnt[0])
    for b in range(4):
        fill(T.ap[0:1, 27 + 32 * b:30 + 32 * b], 1.0)
    if is_rank:
        fill(T.ids[:, 0:1], 1.0)
    fill(T.gm[:, :], 0.0)
    ncs = cnt[0]
    V.wait_ge(sem.cs, ncs)
    if is_rank:
        V.wait_ge(sem.gl, 12)
        V.tensor_copy(T.xg[:, 512:640], pgl).then_inc(sem.gs, 1)
        S.wait_ge(sem.cs, ncs)
        S.dma_start(T.idd[:, :], T.ids[:, :]).then_inc(sem.i1, 16)
        S.wait_ge(sem.i1, 16)
        S.dma_start(T.ident[:, :], T.idd[0:128, :]).then_inc(sem.i2, 16)
    PE.wait_ge(sem.cs, ncs)
    for k, (e, hp) in enumerate(L):
        PE.matmul(pg[k // 4][:, (k % 4) * 128:(k % 4) * 128 + 128], T.ap[0:1, 27 - 3 * e:155 - 3 * e], T.one[0:1, :],
                  True, True).then_inc(sem.se, 1)
    V.wait_ge(sem.se, n)
    nb = (n + 3) // 4
    for b in range(nb):
        w = min(4, n - 4 * b) * 128
        V.tensor_copy(T.sel[:, b * 512:b * 512 + w], pg[b][:, 0:w]).then_inc(sem.sv, 1)
    tot = n + (nh if is_rank else 0)
    done = [0, 0]

    def acc(f, lhsT, rhs):
        PE.matmul(py[f][:, 0:HW], lhsT, rhs, done[f] == 0, done[f] == tot - 1).then_inc(sem["m2%d" % f], 1)
        done[f] += 1

    def mm1(k):
        e, hp = L[k]
        if hp == 0:
            PE.wait_ge(sem.ldw, 32)
        else:
            PE.wait_ge(sem["w%d" % e], 8)
        for f in range(2):
            if k >= 1:
                PE.wait_ge(sem["rl_%d_%d" % (k - 1, f)], 1)
            PE.matmul(ph[f][:, 0:HW], T.wt[:, e * 256:e * 256 + 128], T.xg[:, f * HW:f * HW + HW],
                      True, True).then_inc(sem["m1_%d_%d" % (k, f)], 1)

    def gb(k):
        PE.matmul(pg[k % NG][:, :], T.sel[:, k * 128:k * 128 + 128], T.gm[:, :], True, True).then_inc(sem["gb_%d" % k], 1)

    def mm2(k):
        e = L[k][0]
        for f in range(2):
            PE.wait_ge(sem["mu_%d_%d" % (k, f)], 1)
            acc(f, T.wt[:, e * 256 + 128:e * 256 + 256], T.sg[:, k * 512 + f * HW:k * 512 + f * HW + HW])
        if k + NG < n:
            gb(k + NG)

    if is_rank:
        PE.wait_ge(sem.ldx, 16)
    else:
        PE.wait_ge(sem.xa, 8)
    for k in range(n1):
        mm1(k)
    PE.wait_ge(sem.gms, 4)
    PE.wait_ge(sem.sv, nb)
    for k in range(min(NG, n)):
        gb(k)
    for k in range(n1):
        mm2(k)
    for k in range(n1, n):
        mm1(k)
        if k - 1 >= n1:
            mm2(k - 1)
    if is_rank:
        PE.wait_ge(sem.i2, 16)
        for j in range(nh):
            PE.wait_ge(sem["pa%d" % j], PENG)
            for f in range(2):
                acc(f, T.ident[:, :], T.part[:, j * 512 + f * HW:j * 512 + f * HW + HW])
    if n1 < n:
        mm2(n - 1)

    for k in range(n):
        for f in range(2):
            A.wait_ge(sem["m1_%d_%d" % (k, f)], 1)
            A.activation(T.rl[:, k * 512 + f * HW:k * 512 + f * HW + HW], ph[f][:, 0:HW],
                         ActivationFunctionType.Relu).then_inc(sem["rl_%d_%d" % (k, f)], 1)

    V.wait_ge(sem.fa, sum(_weng(P, c) for c in P["wh"][r] if c != core))
    if hv:
        V.wait_ge(sem.hv, hv)
    if is_rank:
        V.wait_ge(sem.gs, 1)
    else:
        V.wait_ge(sem.xa, 8)
    V.tensor_tensor(T.gd[:, :], T.fb[:, :], T.xg[:, 512:640], AluOpType.mult).then_inc(sem.gp, 1)
    V.wait_ge(sem.gp, 1)
    for b in range(4):
        V.tensor_copy(T.gm[32 * b:32 * b + 32, 128 * b:128 * b + 128], T.gd[32 * b:32 * b + 32, :]).then_inc(sem.gms, 1)
    for k in range(n):
        V.wait_ge(sem["gb_%d" % k], 1)
        for f in range(2):
            V.wait_ge(sem["rl_%d_%d" % (k, f)], 1)
            V.tensor_tensor(T.sg[:, k * 512 + f * HW:k * 512 + f * HW + HW], T.rl[:, k * 512 + f * HW:k * 512 + f * HW + HW],
                            pg[k % NG][:, f * HW:f * HW + HW], AluOpType.mult).then_inc(sem["mu_%d_%d" % (k, f)], 1)
    V.wait_ge(sem.m20, tot)
    V.tensor_copy(T.yo[:, 0:HW], T.py0[:, 0:HW]).then_inc(sem.ev0, 1)
    A.wait_ge(sem.m21, tot)
    A.activation(T.yo[:, HW:2 * HW], T.py1[:, 0:HW], ActivationFunctionType.Copy).then_inc(sem.ev1, 1)
    if is_rank:
        S.wait_ge(sem.ev0, 1)
        S.dma_start(T.y[:, 0:HW], T.yo[:, 0:HW]).then_inc(sem.st, 16)
        A.wait_ge(sem.ev1, 1)
        A.dma_start(T.y[:, HW:2 * HW], T.yo[:, HW:2 * HW]).then_inc(sem.st, 16)
        S.wait_ge(sem.st, 32)
    else:
        rid, pid = topo.addr(R, core)
        g.wait_ge(sem.ev0, 1)
        g.wait_ge(sem.ev1, 1)
        g.remote_dma(T.part[:, h * 512:h * 512 + 512], T.yo[:, :], sem["pa%d" % h], sem.loc, pid, rid,
                     _pick(topo.mask(core, R), PENG))
        loc += PENG
    g.wait_ge(sem.loc, loc)


def rank_program(g, core, T, topo):
    P = _plan(T, topo)
    if core not in P["role"]:
        return
    kind, r, i = P["role"][core]
    if kind == "relay":
        _relay(g, core, T, topo, P, r, i)
    elif kind == "word":
        g.wait_ge(T.sem.loc, _words_send(g, core, T, topo, P, r, _words_vec(g, core, T, P, r, False)))
    else:
        _compute(g, core, T, topo, P, r, i)
